import numpy as np, ml_dtypes
CORES = [24,25,26,27,28,29,30,31]
N = 8
BF = ml_dtypes.bfloat16
M, C, W, RO = 128, 32, 8192, 5
TOP = 255 * N * C
def settle(rng, e):
    x = np.add.accumulate(e, axis=3); x = x - np.min(x, axis=3, keepdims=True); top = np.max(x, axis=3, keepdims=True)
    return x + 32 + (rng.random(top.shape) * (169 - top)).astype(np.int64)
def parts(rng):
    e = rng.integers(-3, 4, (8, 16, M, 8)); x = settle(rng, rng.permuted(np.concatenate([e, -e], axis=3), axis=3))
    s = np.argsort(rng.random((8, 16, M)), axis=1); miss = rng.integers(0, 16, (8, M))
    u = N * C * 127 + rng.integers(-600, 601, (8, 16, M))
    return x, s, miss, u, rng.integers(0, 256, (N, 8, 16, W)), rng.integers(0, 128, (N, 8, 16, C))
def pack(x, s, miss, u, d, a):
    n = np.where(np.arange(16)[:, None] == miss[:, None, :], -1, s)
    def same(y): return np.repeat(np.ascontiguousarray(y).reshape(1, 128, -1), N, axis=0)
    return {"v": same(x).astype(np.float32).astype(BF), "inv": same(n).astype(np.int32), "sup": same(u).astype(np.int32),
            "dem": d.reshape(N, 128, W).astype(np.float32).astype(BF), "wt": np.ascontiguousarray(a).reshape(N, 128, C).astype(np.float32).astype(BF)}
def newcomer(s, miss):
    return np.take_along_axis(s, miss[:, None, :], 1)[:, 0]
def climb(rng, x, s, miss, u, d, a, g):
    o = rng.permutation(16); turn = rng.integers(0, 16, M); j = (np.arange(16) - turn[:, None]) % 16
    key = int(rng.integers(0, 16)); b = int(rng.integers(32, 177))
    far = np.where(rng.random((16, M, 1)) < 0.5, 32 + 3 * (j & 1), 200 - 3 * (j & 1))
    x[g] = np.where(rng.random((16, M, 1)) < 0.5, far, x[g]); x[g, key] = b + 3 * np.minimum(j, 16 - j)
    t = np.zeros((16, M), np.int64); t[o[:5]] = np.arange(1, 6)[:, None]
    t[o[5:]] = rng.permuted(np.repeat(np.array([0, 6, 7, 8, 9, 10, 11, 12, 13, 14, 15])[:, None], M, axis=1), axis=0)
    s[g] = (t + turn) % 16; miss[g] = np.argmax(t == 8, axis=0)
    u[g] = rng.integers(0, 128 * N * C, (16, M)); d[:, g] = rng.integers(0, 64, (N, 16, W)); a[:, g] = 0; a[:, g, key] = 1
    at = [-1] + [int(y) for y in o[:5]] + [-1] * 10; c = 8
    for w in [int(y) for y in rng.permutation(np.array([1, 3, 5]))] + [int(y) for y in rng.permutation(np.array([2, 4]))] + [3]:
        d[:, g, at[w], b + 3 * c] = 255; at[c] = at[w]; c = w
def setup_inputs(rng):
    return pack(*parts(rng))
def setup_inputs_alike(rng):
    x, s, miss, u, d, a = parts(rng)
    for g in (0, 2, 5, 7): x[g] = x[g][:, :1]; s[g] = s[g][:, :1]; miss[g] = miss[g, 0]; u[g] = u[g][:, :1]
    for g in (1, 2, 6, 7): a[:, g] = a[:, g, :, :1]
    for y in (d, a): y[:, 3] = y[:1, 3].copy(); y[1, 4] = y[0, 4]
    return pack(x, s, miss, u, d, a)
def setup_inputs_ends(rng):
    x, s, miss, u, d, a = parts(rng)
    e = rng.permuted(np.broadcast_to(np.repeat(np.array([3, -3]), 8), (8, 16, M, 16)).copy(), axis=3); e[:, ::2] = np.sort(e[:, ::2], axis=3)
    x = np.add.accumulate(e, axis=3); x = x - np.min(x, axis=3, keepdims=True); top = np.max(x, axis=3, keepdims=True)
    low = rng.random(top.shape) < 0.5; low[3] = False
    x = x + np.where(low, 32, 200 - top); c = newcomer(s, miss)
    for g in range(8):
        for i in (14, 15): x[g, i, 0] += 50 + i - x[g, i, 0, c[g, 0]]
    a = 127 * rng.integers(0, 2, a.shape); a[..., 0] = 0; a[..., 3] = 0; a[:, :, 5, 3] = 1
    a[:, 3, :, 4:] = 127 - rng.integers(0, 16, (N, 16, C - 4)); a[:, 3, :, 4] = 127
    for r in range(N):
        for g in range(8):
            p = x[g, :, 0, c[g, 0]]
            for j, t in ((1, W - 1), (2, 0)):
                b = rng.integers(0, 128, 16); k = int(t - np.sum(b[:14] * p[:14])) % W
                b[15] = k % 64; b[14] = (k // 64 - k % 64) % (W // 64); a[r, g, :, j] = b
    d[..., 0] = 255 * rng.integers(0, 2, (N, 8, 16)); d[..., W - 1] = 255 * rng.integers(0, 2, (N, 8, 16))
    m = rng.integers(0, 600, (8, 16, M)); u = np.where(rng.random((8, 1, M)) < 0.5, m, TOP - m)
    few = rng.integers(0, 3, (2, 16, M)) * (rng.random((2, 1, M)) < 0.5)
    d[:, 1, :, :W - 1] = 255 - (rng.random((N, 16, W - 1)) < 1.0 / C); u[1] = few[0]
    d[:, 4, :, :W - 1] = rng.integers(200, 256, (N, 16, W - 1)); u[4] = rng.integers(0, 256, (16, M))
    d[:, 6, :, :W - 1] = rng.random((N, 16, W - 1)) < 1.0 / C; u[6] = TOP - few[1]
    climb(rng, x, s, miss, u, d, a, 7)
    return pack(x, s, miss, u, d, a)
def setup_inputs_rest(rng):
    x, s, miss, u, d, a = parts(rng); d = rng.integers(1, 255, d.shape); c = newcomer(s, miss)
    kind = rng.integers(0, 4, (8, M)); kind[0] = 0; kind[1] = rng.integers(1, 3, M)
    end = np.where(rng.random((8, M)) < 0.5, 0, 15); end = np.where(end == c, 15 - end, end)
    near = (c + np.where(rng.random((8, M)) < 0.5, 1, 15)) % 16
    want = np.where(kind == 0, c, np.where(kind == 1, end, near))
    fav = np.take_along_axis(np.argsort(s, axis=1), want[:, None, :], 1)
    lab = rng.integers(0, 16, (8, 1, M)); lab[1:] = int(rng.integers(0, 16))
    s = np.take_along_axis(s, (np.arange(16)[:, None] + fav - lab) % 16, 1); miss = (miss - (fav - lab)[:, 0]) % 16
    u = np.where((kind == 3)[:, None, :], u, np.where(np.arange(16)[:, None] == lab, 0, TOP))
    return pack(x, s, miss, u, d, a)
def setup_inputs_ties(rng):
    x, s, miss, u, d, a = parts(rng)
    d = 255 * (rng.random(d.shape) < 1.0 / (N * C)).astype(np.int64); d[:, 3] = 0
    u = np.repeat(255 * rng.choice(np.array([0, 1, N * C // 2, N * C - 1]), (8, 1, M)), 16, axis=1)
    u[::2] = u[::2] + 255 * rng.integers(0, 2, u[::2].shape)
    u[3] = 255 * rng.choice(np.array([0, 1, N * C // 2, N * C]), (1, M))
    return pack(x, s, miss, u, d, a)
def setup_inputs_spread(rng):
    x, s, miss, u, d, a = parts(rng)
    d = (np.exp2(8 * rng.random((N, 8, 1, W))) * rng.random(d.shape)).astype(np.int64)
    a = np.exp2(7 * rng.random(a.shape)).astype(np.int64) * (rng.random(a.shape) > 0.0625)
    return pack(x, s, miss, rng.integers(0, 2 * N * C, u.shape), d, a)
def check_inputs(d):
    bad = []
    for k, lo, hi in (("v", 32, 200), ("sup", 0, TOP), ("dem", 0, 255), ("wt", 0, 127)):
        y = np.asarray(d[k]).astype(np.float64)
        if not np.all((y >= lo) & (y <= hi) & (y == np.floor(y))): bad.append("range of " + k)
    x = np.asarray(d["v"]).astype(np.float64).reshape(N, 8, 16, M, 16)
    if not np.all(np.abs(np.roll(x, -1, axis=4) - x) <= 3): bad.append("ring neighbours in v")
    s = np.sort(np.asarray(d["inv"]).astype(np.int64).reshape(N, 8, 16, M), axis=2)
    if not (np.all(s[:, :, 0] == -1) and np.all(s[:, :, 1] >= 0) and np.all(s[:, :, 15] <= 15) and np.all(s[:, :, 1:] > s[:, :, :-1])): bad.append("slots in inv")
    for k in ("v", "inv", "sup"):
        y = np.asarray(d[k]).astype(np.float64)
        if not np.all(y == y[:1]): bad.append(k + " is not the same on all ranks")
    return bad
def reference(v, inv, sup, dem, wt):
    x = v[0].astype(np.float32).astype(np.int64).reshape(8, 16, M, 16); n = inv[0].astype(np.int64).reshape(8, 16, M); u = sup[0].astype(np.int64).reshape(8, 16, M)
    d = dem.astype(np.float32).astype(np.int64).reshape(N, 8, 16, W); a = wt.astype(np.float32).astype(np.int64).reshape(N, 8, 16, C).transpose(0, 1, 3, 2)
    row = np.arange(16)[:, None]; slot = np.arange(16)
    def pick(k): return np.take_along_axis(x, (k & 15)[:, None, :, None], 3)[..., 0]
    c = 119 - np.add.reduce(n, axis=1)
    for step in range(RO):
        p = pick(c)
        h = np.matmul(a, p[None]) & (W - 1)
        z = np.add.reduce(np.take_along_axis(d, h.reshape(N, 8, 1, C * M), 3).reshape(N, 8, 16, C, M), axis=(0, 3)) - u
        l = np.argmax(z, axis=1)
        s = np.take_along_axis(n, l[:, None, :], 1)[:, 0]; go = s >= 0
        new = pick(s - 1) + pick(s + 1) - pick(s)
        x = np.where((slot == s[:, None, :, None]) & go[:, None, :, None], new[..., None], x)
        n = np.where((row == l[:, None, :]) & go[:, None, :], c[:, None, :], n)
        c = np.where(go, s, c)
    return {"yv": np.repeat(x.reshape(1, 128, 16 * M), N, axis=0).astype(np.float32).astype(BF), "yi": np.repeat(n.reshape(1, 128, M), N, axis=0).astype(np.float32)}

@@ -1,0 +1,329 @@
+from concourse.bass import DstId, RemoteDMATransfer
+from concourse.mybir import AluOpType as A, AxisListType, ActivationFunctionType as F
+
+N, STEPS = 8, 5
+VWID, SPARE = 288, 258
+FIRST = (((0, 64), (64, 96), (96, 128)), ((192, 256), (160, 192), (128, 160)),
+         ((0, 64), (192, 256), (64, 96), (160, 192), (96, 128), (128, 160)))
+LATER = (((0, 64), (64, 96), (96, 128), (128, 150)), ((192, 256), (160, 192), (150, 160)),
+         ((0, 64), (64, 96), (192, 256), (96, 128), (160, 192), (128, 160)))
+BF, FP, I32, U16 = "bfloat16", "float32", "int32", "uint16"
+SCRATCH = {"stage": ("dram", [N, 128, 1024], BF), "tl": ("dram", [N, 128, 1024], BF), "ws": ("dram", [N, 128, 4], BF),
+           "wd": ("dram", [N, 128, 4], BF), "dv": ("dram", [N, 128, 256], BF), "dn": ("dram", [N, 128, 16], FP)}
+for _dt, _bufs in ((BF, dict(Y=8192, G=4096, wx=32, wl=256, wr=256, Wm=2048, v0=256, VW=VWID, NW=VWID, invb=128, suph=128,
+                             supl=128, eye=128, neye=128, turn=128, unturn=128, rep=128, R=32, Rh=32, Rl=32, pay=48,
+                             new=16, dl=16, ex=128, vt=256)),
+                   (FP, dict(tf=128, jm=128, jd=128, jp=128, jq=128, pc=16, mk=8, cut=32, tie=16, xf=8, sc=32, sv=8,
+                             ns=8, na=8, dd=8, nt=16)),
+                   (I32, dict(invi=128, supi=128, ti=128, pi=8, h1=256, h2=256)),
+                   (U16, dict(xo=8, off=256, pick=2, tgt=2))):
+    for _name, _cols in _bufs.items():
+        SCRATCH[_name] = ("sbuf", [128, _cols], _dt)
+PSUM = ("ha", "hb", "key", "m0", "m1", "m2")
+for _name in PSUM:
+    SCRATCH[_name] = ("psum", [128, 512], FP)
+SEMAPHORES = (["cg", "cv", "cs", "ct", "sent", "aw", "av", "an"] + ["at%d" % s for s in range(N)]
+              + ["d%d" % k for k in range(32)])
+
+
+def make_sched(g, T):
+    queue = {"g": g, "v": g.vector, "s": g.scalar, "t": g.tensor, "y": g.sync}
+    counter = {"g": "cg", "v": "cv", "s": "cs", "t": "ct"}
+    total, known, writer, readers, ndma = {}, {q: {} for q in queue}, {}, {}, [0]
+
+    def order(q, reads, writes):
+        toks = []
+        for k in reads:
+            if k in writer:
+                toks.append(writer[k])
+            if k in PSUM:
+                toks += [tok for tok in readers.get(k, []) if tok[3] != q]
+        for k in writes:
+            if k in writer:
+                toks.append(writer[k])
+            toks += readers.get(k, [])
+        toks = [tok for tok in toks if not (q == "t" and tok[3] == "t")]
+        for sem, val, clock, src in sorted(toks, key=lambda tok: -sum(tok[2].values())):
+            if known[q].get(sem, 0) < val:
+                queue[q].wait_ge(T.sem[sem], val)
+            for k, x in clock.items():
+                if known[q].get(k, 0) < x:
+                    known[q][k] = x
+
+    def done(q, sem, n, reads, writes, src):
+        total[sem] = total.get(sem, 0) + n
+        clock = dict(known[q]); clock[sem] = total[sem]
+        tok = (sem, total[sem], clock, src)
+        for k in reads:
+            readers.setdefault(k, []).append(tok)
+        for k in writes:
+            writer[k] = tok; readers[k] = []
+
+    def op(q, call, reads, writes):
+        order(q, reads, writes)
+        call().then_inc(T.sem[counter[q]], 1)
+        done(q, counter[q], 1, reads, writes, q)
+
+    def dma(q, out, in_, reads, writes):
+        order(q, reads, writes)
+        sem = "d%d" % ndma[0]; ndma[0] += 1
+        queue[q].dma_start(out, in_).then_inc(T.sem[sem], 16)
+        done(q, sem, 16, reads, writes, "dma")
+
+    def remote(call, n, reads):
+        order("g", reads, [])
+        call()
+        total["sent"] = total.get("sent", 0) + n
+
+    def lands(key, sem, n):
+        total[sem] = n
+        writer[key] = (sem, n, {sem: n}, "far")
+
+    def finish():
+        for sem, n in total.items():
+            if known["g"].get(sem, 0) < n:
+                g.wait_ge(T.sem[sem], n)
+
+    return op, dma, remote, lands, finish
+
+
+def rank_program(g, core, T, topo):
+    r = T.rank_of(core)
+    if r is None:
+        return
+    op, dma, remote, lands, finish = make_sched(g, T)
+    V, S, P = g.vector, g.scalar, g.tensor
+    cores = T.cores
+    near = [s for s in range(N) if topo.die(cores[s]) == topo.die(core)]
+    far = [s for s in range(N) if topo.die(cores[s]) != topo.die(core)]
+    me = near.index(r)
+    far_to = [far[(me + k) % len(far)] for k in range(len(far))]
+    near_to = [near[(me + k) % len(near)] for k in range(1, len(near))]
+    far_from = [far[(me - k) % len(far)] for k in range(len(far))]
+    near_from = [near[(me - k) % len(near)] for k in range(1, len(near))]
+    eng = topo.engines(core, cores[far[0]])
+    mask = [sum(1 << e for e in h) for h in (eng[0::2], eng[1::2])]
+    E = len(eng) // 2
+
+    def dst(s):
+        rid, pid, _ = topo.addr(cores[s])
+        return DstId(rid=rid, pnc=pid)
+
+    def to_all(src, land, sem, reads, flip):
+        ts = [RemoteDMATransfer(dst_ids=[dst(s) for s in to], dma_engine_mask=mask[k ^ flip], remote_sem=T.sem[sem],
+                                srcs=[src], dsts=[land for _ in to]) for k, to in enumerate((far_to, near_to))]
+        remote(lambda: g.remote_dma_fused(ts, local_sem=T.sem.sent), 2 * E, reads)
+
+    def ts(out, in0, s1, s2, op0, op1, reads, writes):
+        if op1 is None:
+            op("v", lambda: V.tensor_scalar(out, in0, s1, None, op0), reads, writes)
+        else:
+            op("v", lambda: V.tensor_scalar(out, in0, s1, s2, op0, op1), reads, writes)
+
+    def tc(out, in_, reads, writes):
+        op("v", lambda: V.tensor_copy(out, in_), reads, writes)
+
+    def tt(out, in0, in1, o, reads, writes):
+        op("v", lambda: V.tensor_tensor(out, in0, in1, o), reads, writes)
+
+    def fill(out, x, key):
+        op("v", lambda: V.memset(out, x), [], [key])
+
+    def act(out, in_, f, reads, writes, **kw):
+        op("s", lambda: S.activation(out, in_, f, **kw), reads, writes)
+
+    def mm(out, lhsT, rhs, start, stop, reads, writes):
+        op("t", lambda: P.matmul(out, lhsT, rhs, start, stop), reads, writes)
+
+    def iota(name, pattern, cm):
+        op("g", lambda: g.iota(T[name][:], pattern, 0, cm, allow_small_or_imprecise_dtypes=True), [], [name])
+
+    rows = slice(16 * r, 16 * r + 16)
+    order_to = [x for k in range(len(far)) for x in ([far_to[k]] + near_to[k:k + 1])]
+    pair = len(eng) // N
+    lands("wd_far", "aw", (N - 1) * pair)
+    lands("dv_far", "av", (N - 1) * E)
+    lands("dn_far", "an", (N - 1) * E)
+    for s in order_to:
+        lands("tl%d" % s, "at%d" % s, E)
+
+    dma("s", T.ws[:], T.wt[:], [], ["ws"])
+    for s in order_to:
+        dma("y", T.stage[s], T.dem[16 * s:16 * s + 16, :], [], ["stage%d" % s])
+    dma("s", T.invi[0:16, :], T.inv[rows, :], [], ["invi"])
+    dma("s", T.v0[:], T.v[rows, :], [], ["v0"])
+    dma("s", T.supi[0:16, :], T.sup[rows, :], [], ["supi"])
+    dma("s", T.wd[r], T.wt[rows, :], [], ["wd_own"])
+
+    op("g", lambda: g.iota(T.pi[:, 0:1], [[0, 1]], 0, 1), [], ["pi0"])
+    iota("jm", [[0, 8], [1, 16]], 0)
+    iota("jd", [[-1, 128]], 1)
+    iota("jq", [[1, 8], [8, 16]], -1)
+    iota("jp", [[1, 16], [16, 8]], -1)
+    wts = [RemoteDMATransfer(dst_ids=[dst(s)], dma_engine_mask=sum(1 << e for e in eng[pair * k:pair * k + pair]),
+                             remote_sem=T.sem.aw, srcs=[T.ws[s]], dsts=[T.wd[r]]) for k, s in enumerate(order_to)]
+    remote(lambda: g.remote_dma_fused(wts, local_sem=T.sem.sent), (N - 1) * pair, ["ws"])
+    for s in order_to:
+        rid, pid, _ = topo.addr(cores[s])
+        m = mask[0 if s in far else 1]
+        remote(lambda: g.remote_dma(T.tl[r], T.stage[s], T.sem["at%d" % r], T.sem.sent, pid, rid, m), E, ["stage%d" % s])
+
+    dma("s", T.wx[:], T.wd[:], ["wd_own", "wd_far"], ["wx"])
+    for k, s in enumerate(near_from):
+        dma("s", T.Y[16 * s:16 * s + 16, :], T.tl[s], ["tl%d" % s], ["Y%d" % s])
+        if k == 0:
+            dma("s", T.Y[rows, :], T.dem[rows, :], [], ["Y%d" % r])
+    for s in far_from:
+        dma("y", T.Y[16 * s:16 * s + 16, :], T.tl[s], ["tl%d" % s], ["Y%d" % s])
+    Yk = ["Y%d" % s for s in range(N)]
+
+    ts(T.pi[:, 1:2], T.pi[:, 0:1], 15, None, A.bitwise_and, None, ["pi0"], ["pi1"])
+    ts(T.pi[:, 2:3], T.pi[:, 0:1], 4, None, A.arith_shift_right, None, ["pi0"], ["pi2"])
+    ts(T.pi[:, 3:4], T.pi[:, 0:1], 7, None, A.bitwise_and, None, ["pi0"], ["pi3"])
+    ts(T.pi[:, 4:5], T.pi[:, 0:1], 3, 1, A.arith_shift_right, A.bitwise_and, ["pi0"], ["pi4"])
+    ts(T.pi[:, 5:6], T.pi[:, 0:1], 3, None, A.arith_shift_right, None, ["pi0"], ["pi5"])
+    tc(T.pc[:, 0:6], T.pi[:, 0:6], ["pi%d" % k for k in range(6)], ["pc"])
+    pc = [T.pc[:, k:k + 1] for k in range(16)]
+    pm, pd, p8, ph, pe, pb = pc[1:7]
+    ts(pb, pm, 16.0, None, A.mult, None, ["pc"], ["pb"])
+    ts(pc[11], pm, -15.0, float(SPARE), A.mult, A.add, ["pc"], ["pc11"])
+    ts(pc[12], pm, float(SPARE), None, A.add, None, ["pc"], ["pc12"])
+    ts(T.rep[:], T.jm[:], pm, None, A.is_equal, None, ["jm", "pc"], ["rep"])
+    for name, x in (("R", 256.0), ("Rh", -65536.0), ("Rl", -256.0)):
+        ts(T[name][:], T.jm[:, 0:32], pm, x, A.is_equal, A.mult, ["jm", "pc"], [name])
+    ts(T.mk[:], T.jm[:, 0:8], pd, None, A.is_equal, None, ["jm", "pc"], ["mk"])
+    ts(T.tie[:], T.jm[:, 0:16], -16.0, 241.0, A.mult, A.add, ["jm"], ["tie"])
+    fill(T.pay[:, 32:48], 0.0, "pay0")
+    ts(T.pay[:, 0:16], T.jm[:, 0:16], -16.0, 240.0, A.mult, A.add, ["jm"], ["pay1"])
+    ts(T.cut[:], T.jm[:, 0:32], 0.0, -1.0e9, A.is_equal, A.mult, ["jm"], ["cut"])
+    fill(T.na[:, 0:1], -1.0, "na0")
+    fill(T.VW[:], 0.0, "VW")
+    fill(T.NW[:], 0.0, "NW")
+    ts(T.neye[:], T.jd[:], 0.0, -1.0, A.is_equal, A.mult, ["jd"], ["neye"])
+    for name, src in (("eye", "jd"), ("unturn", "jq"), ("turn", "jp")):
+        ts(T[name][:], T[src][:], 0.0, None, A.is_equal, None, [src], [name])
+    ts(pc[7], p8, pd, None, A.is_equal, None, ["pc"], ["pc7"])
+    ts(pc[8], ph, -16.0, None, A.add, None, ["pc"], ["pc8"])
+    ts(T.xf[:], T.jm[:, 0:8], 2.0, pc[8], A.mult, A.add, ["jm", "pc8"], ["xf"])
+    ts(T.xo[:], T.xf[:], pc[7], 32.0, A.mult, A.add, ["xf", "pc7"], ["xo"])
+    ts(pc[9], pe, 16.0, -241.0, A.mult, A.add, ["pc"], ["pc9"])
+
+    tc(T.tf[0:16, :], T.invi[0:16, :], ["invi"], ["tf"])
+    tc(T.invb[0:16, :], T.tf[0:16, :], ["tf"], ["invb"])
+    mm(T.m0[:, 0:16], T.invb[0:16, :], T.rep[0:16, 0:16], True, True, ["invb", "rep"], ["m0"])
+    mm(T.m1[:, 0:256], T.unturn[:], T.v0[:], True, True, ["unturn", "v0"], ["m1"])
+    tt(T.pay[:, 16:32], T.m0[:, 0:16], T.tie[:], A.add, ["m0", "tie", "pay0", "pay1"], ["pay"])
+    op("v", lambda: V.tensor_reduce(pc[10], T.m0[:, 0:16], AxisListType.X, A.add), ["m0"], ["pc10"])
+    ts(T.ns[:, 0:1], pc[10], -120.0, None, A.add, None, ["pc10"], ["ns0"])
+    ts(T.tgt[:, 0:1], T.ns[:, 0:1], -1.0, pb, A.mult, A.add, ["ns0", "pb"], ["tgt"])
+    tc(T.VW[:, 1:257], T.m1[:, 0:256], ["m1"], ["VW"])
+    tc(T.new[:], T.VW[:].indirect(T.tgt[:, 0:1]), ["VW", "tgt"], ["new"])
+    for name, o, x in (("suph", A.arith_shift_right, 8), ("supl", A.bitwise_and, 255)):
+        ts(T.ti[0:16, :], T.supi[0:16, :], x, None, o, None, ["supi"], ["ti"])
+        tc(T.tf[0:16, :], T.ti[0:16, :], ["ti"], ["tf"])
+        tc(T[name][0:16, :], T.tf[0:16, :], ["tf"], [name])
+    for s in range(N):
+        ts(T.wl[:, 32 * s:32 * s + 32], T.wx[:], T.mk[:, s:s + 1], None, A.mult, None, ["wx", "mk"], ["wl%d" % s])
+    mm(T.m2[:, 0:256], T.rep[:], T.wl[:], True, True, ["rep"] + ["wl%d" % s for s in range(N)], ["m2"])
+    for eh in range(2):
+        tc(T.wr[:, 128 * eh:128 * eh + 128], T.m2[:, eh:256:2], ["m2"], ["wr%d" % eh])
+    for qh in range(8):
+        ts(T.Wm[:, 256 * qh:256 * qh + 256], T.wr[:], T.mk[:, qh:qh + 1], None, A.mult, None, ["wr0", "wr1", "mk"], ["Wm%d" % qh])
+
+    def places(piece, stage):
+        a, b = ((0, 64), (64, 256))[piece]
+        bank = ("ha", "hb")[piece]
+        if stage == 0:
+            tc(T.h1[:, a:b], T[bank][:, 0:b - a], [bank], ["h1%d" % piece])
+        elif stage == 1:
+            ts(T.h2[:, a:b], T.h1[:, a:b], 8191, None, A.bitwise_and, None, ["h1%d" % piece], ["h2%d" % piece])
+        else:
+            tc(T.off[:, a:b], T.h2[:, a:b], ["h2%d" % piece], ["off%d" % piece])
+
+    m0c, mcc = T.sc[:, 15:16], T.sc[:, 31:32]
+
+    def book(t, what):
+        ns, np_, na, nap = T.ns[:, t + 1:t + 2], T.ns[:, t:t + 1], T.na[:, t + 1:t + 2], T.na[:, t:t + 1]
+        kns, knp, kna, knap = "ns%d" % (t + 1), "ns%d" % t, "na%d" % (t + 1), "na%d" % t
+        if what == "ns":
+            ts(ns, mcc, m0c, nap, A.subtract, A.mult, ["sc", knap], [kns])
+        elif what == "flags":
+            act(na, ns, F.Sign, [kns], [kna])
+            act(T.dd[:, 0:1], np_, F.Identity, [knp, kna, kns], ["dd"], bias=ns, scale=na)
+            act(T.sv[:, 0:1], na, F.Identity, [kna, "pc11", "pc12"], ["sv"], bias=pc[12], scale=pc[11])
+        elif what == "tgt":
+            ts(T.tgt[:, 0:1], T.sv[:, 0:1], ns, None, A.subtract, None, [kns, "sv"], ["tgt"])
+        elif what == "put":
+            tc(T.VW[:].indirect(T.tgt[:, 0:1]), T.new[:], ["tgt", "new"], ["VW"])
+        elif what == "dl":
+            ts(T.dl[:], T.key[:, 0:16], m0c, T.dd[:, 0:1], A.is_equal, A.mult, ["key", "sc", "dd"], ["dl"])
+        else:
+            tt(T.pay[:, 16:32], T.pay[:, 16:32], T.dl[:], A.add, ["pay", "dl"], ["pay"])
+
+    def mirror():
+        for out, eye, src, st in ((slice(0, 256), "neye", slice(1, 257), 0), (slice(0, 256, 16), "eye", slice(16, 257, 16), 1),
+                                  (slice(0, 256, 16), "neye", slice(0, 256, 16), 1), (slice(15, 256, 16), "eye", slice(1, 257, 16), 1),
+                                  (slice(15, 256, 16), "neye", slice(17, 258, 16), 1), (slice(0, 256), "eye", slice(0, 256), 1),
+                                  (slice(0, 256), "eye", slice(2, 258), 2)):
+            mm(T.m2[:, out], T[eye][:], T.VW[:, src], st == 0, st == 2, [eye, "VW"], ["m2"])
+
+    for t in range(STEPS):
+        for eh in range(2):
+            for qh in range(8):
+                c = 128 * eh + 16 * qh
+                bank, c0 = ("ha", c) if c < 64 else ("hb", c - 64)
+                w = 256 * qh + 128 * eh
+                mm(T[bank][:, c0:c0 + 16], T.Wm[:, w:w + 128], T.new[:], True, True, ["Wm%d" % qh, "new"], [bank])
+        for k in range(3):
+            places(0, k)
+        if t:
+            book(t - 1, "tgt")
+        for k in range(3):
+            places(1, k)
+            if t:
+                book(t - 1, ("put", "dl", "pay")[k])
+        mirror()
+        on_s, on_v, sums = LATER if t else FIRST
+        for q, calls in (("s", on_s), ("v", on_v)):
+            for a, b in calls:
+                out, src = T.G[:, 16 * a:16 * b], T.Y[:].indirect(T.off[:, a:b])
+                reads, writes = Yk + ["off%d" % (0 if b <= 64 else 1)], ["G%d" % c for c in range(a // 2, b // 2)]
+                if q == "s":
+                    act(out, src, F.Copy, reads, writes)
+                else:
+                    tc(out, src, reads, writes)
+        act(T.NW[:, 1:257], T.m2[:, 0:256], F.Copy, ["m2"], ["NW"])
+        mm(T.key[:, 0:32], T.suph[0:16, :], T.Rh[0:16, :], True, False, ["suph", "Rh"], ["key"])
+        mm(T.key[:, 0:32], T.supl[0:16, :], T.Rl[0:16, :], False, False, ["supl", "Rl"], ["key"])
+        for a, b in sums:
+            for e in range(16):
+                mm(T.key[a % 128:a % 128 + b - a, 0:32], T.G[:, 16 * a + e:16 * b:16], T.R[:], False, False,
+                   ["G%d" % c for c in range(a // 2, b // 2)] + ["R"], ["key"])
+        mm(T.key[:, 0:32], T.eye[:], T.pay[:, 0:32], False, True, ["eye", "pay"], ["key"])
+        op("v", lambda: V.tensor_tensor_scan(T.sc[:], T.cut[:], T.key[:, 0:32], -1.0e9, A.add, A.max), ["cut", "key"], ["sc"])
+        if t < STEPS - 1:
+            ts(T.pick[:, 0:1], mcc, m0c, pb, A.subtract, A.add, ["sc", "pb"], ["pick"])
+            book(t, "ns")
+        else:
+            book(t, "ns")
+            ts(T.pick[:, 0:1], mcc, m0c, pb, A.subtract, A.add, ["sc", "pb"], ["pick"])
+        tc(T.new[:], T.NW[:].indirect(T.pick[:, 0:1]), ["NW", "pick"], ["new"])
+        book(t, "flags")
+
+    for what in ("dl", "tgt", "pay", "put"):
+        book(STEPS - 1, what)
+    tc(T.ex[:], T.pay[:].indirect(T.xo[:]), ["pay", "xo"], ["ex"])
+    mm(T.m1[:, 0:256], T.turn[:], T.VW[:, 1:257], True, True, ["turn", "VW"], ["m1"])
+    mm(T.m0[:, 0:16], T.ex[:], T.rep[:, 0:16], True, True, ["ex", "rep"], ["m0"])
+    act(T.vt[:], T.m1[:, 0:256], F.Copy, ["m1"], ["vt"])
+    ts(T.nt[:], T.m0[:, 0:16], pc[9], None, A.add, None, ["m0", "pc9"], ["nt"])
+    dma("y", T.dn[r], T.nt[:], ["nt"], ["dn_own"])
+    to_all(T.vt[:], T.dv[r], "av", ["vt", "nt"], 0)
+    to_all(T.dn[r], T.dn[r], "an", ["dn_own"], 1)
+    dma("s", T.yv[rows, :], T.vt[:], ["vt", "dn_own"], ["yv_own"])
+    if r > 0:
+        dma("y", T.yv[0:16 * r, :], T.dv[0:r], ["dv_far"], ["yv_a"])
+    if r < N - 1:
+        dma("s" if r > 0 else "y", T.yv[16 * r + 16:128, :], T.dv[r + 1:N], ["dv_far"], ["yv_b"])
+    dma("y" if 0 < r < N - 1 else "s", T.yi[:], T.dn[:], ["dn_own", "dn_far"], ["yi"])
+    finish()

@@ -3,23 +3,27 @@ from concourse.mybir import AluOpType as A, AxisListType, ActivationFunctionType
 
 N, STEPS = 8, 5
 VWID, SPARE = 288, 258
-FIRST = (((0, 64), (64, 96), (96, 128)), ((192, 256), (160, 192), (128, 160)),
-         ((0, 64), (192, 256), (64, 96), (160, 192), (96, 128), (128, 160)))
-LATER = (((0, 64), (64, 96), (96, 128), (128, 150)), ((192, 256), (160, 192), (150, 160)),
-         ((0, 64), (64, 96), (192, 256), (96, 128), (160, 192), (128, 160)))
+BIG = 1.5 * 2.0 ** 36
+PIECES = ((0, 76), (76, 256))
+ON_V = ("spare", "new", ("u", 0), "tgt", ("u", 1), "put", "dl", ("g", 76, 128), "pay", ("g", 176, 224), ("g", 238, 256))
+ON_S = ((0, 76), (128, 176), (224, 238))
+SUMS = ((0, 128), (128, 224), (224, 256))
+FIRST_V = (("g", 64, 128), ("g", 176, 224), ("g", 240, 256))
+FIRST_S = ((0, 64), (128, 176), (224, 240))
+FIRST_SUMS = SUMS
 BF, FP, I32, U16 = "bfloat16", "float32", "int32", "uint16"
 SCRATCH = {"stage": ("dram", [N, 128, 1024], BF), "tl": ("dram", [N, 128, 1024], BF), "ws": ("dram", [N, 128, 4], BF),
            "wd": ("dram", [N, 128, 4], BF), "dv": ("dram", [N, 128, 256], BF), "dn": ("dram", [N, 128, 16], FP)}
-for _dt, _bufs in ((BF, dict(Y=8192, G=4096, wx=32, wl=256, wr=256, Wm=2048, v0=256, VW=VWID, NW=VWID, invb=128, suph=128,
-                             supl=128, eye=128, neye=128, turn=128, unturn=128, rep=128, R=32, Rh=32, Rl=32, pay=48,
-                             new=16, dl=16, ex=128, vt=256)),
-                   (FP, dict(tf=128, jm=128, jd=128, jp=128, jq=128, pc=16, mk=8, cut=32, tie=16, xf=8, sc=32, sv=8,
-                             ns=8, na=8, dd=8, nt=16)),
-                   (I32, dict(invi=128, supi=128, ti=128, pi=8, h1=256, h2=256)),
-                   (U16, dict(xo=8, off=256, pick=2, tgt=2))):
+for _dt, _bufs in ((BF, dict(Y=8192, G=4096, wx=32, wl=256, wr=256, wn=256, wide=128, v0=256, VW=VWID, NW=VWID, invb=128,
+                             suph=128, supl=128, eye=128, neye=128, turn=128, unturn=128, rep=128, R=32, Rh=32, Rl=32,
+                             pay=32, new=16, dl=16, vt=256, one=128, cst=1024)),
+                   (FP, dict(tf=128, jm=128, jd=128, jp=128, jq=128, pc=16, mk=8, cut=32, tie=16, sc=32, sv=8,
+                             ns=8, na=8, dd=8, nt=128, own=8)),
+                   (I32, dict(invi=128, supi=128, ti=128, pi=8)),
+                   (U16, dict(off=256, pick=2, tgt=2, pick8=8))):
     for _name, _cols in _bufs.items():
         SCRATCH[_name] = ("sbuf", [128, _cols], _dt)
-PSUM = ("ha", "hb", "key", "m0", "m1", "m2")
+PSUM = ("x0", "x1", "x2", "x3", "key", "m0", "m1", "m2")
 for _name in PSUM:
     SCRATCH[_name] = ("psum", [128, 512], FP)
 SEMAPHORES = (["cg", "cv", "cs", "ct", "sent", "aw", "av", "an"] + ["at%d" % s for s in range(N)]
@@ -179,66 +183,87 @@ def rank_program(g, core, T, topo):
 
     ts(T.pi[:, 1:2], T.pi[:, 0:1], 15, None, A.bitwise_and, None, ["pi0"], ["pi1"])
     ts(T.pi[:, 2:3], T.pi[:, 0:1], 4, None, A.arith_shift_right, None, ["pi0"], ["pi2"])
-    ts(T.pi[:, 3:4], T.pi[:, 0:1], 7, None, A.bitwise_and, None, ["pi0"], ["pi3"])
-    ts(T.pi[:, 4:5], T.pi[:, 0:1], 3, 1, A.arith_shift_right, A.bitwise_and, ["pi0"], ["pi4"])
-    ts(T.pi[:, 5:6], T.pi[:, 0:1], 3, None, A.arith_shift_right, None, ["pi0"], ["pi5"])
-    tc(T.pc[:, 0:6], T.pi[:, 0:6], ["pi%d" % k for k in range(6)], ["pc"])
+    tc(T.pc[:, 0:3], T.pi[:, 0:3], ["pi%d" % k for k in range(3)], ["pc"])
     pc = [T.pc[:, k:k + 1] for k in range(16)]
-    pm, pd, p8, ph, pe, pb = pc[1:7]
+    pm, pd, pb, gap, untie, tot = pc[1:7]
     ts(pb, pm, 16.0, None, A.mult, None, ["pc"], ["pb"])
-    ts(pc[11], pm, -15.0, float(SPARE), A.mult, A.add, ["pc"], ["pc11"])
-    ts(pc[12], pm, float(SPARE), None, A.add, None, ["pc"], ["pc12"])
+    ts(gap, pm, -15.0, float(SPARE), A.mult, A.add, ["pc"], ["gap"])
+    ts(untie, pm, 16.0, -241.0, A.mult, A.add, ["pc"], ["untie"])
     ts(T.rep[:], T.jm[:], pm, None, A.is_equal, None, ["jm", "pc"], ["rep"])
     for name, x in (("R", 256.0), ("Rh", -65536.0), ("Rl", -256.0)):
         ts(T[name][:], T.jm[:, 0:32], pm, x, A.is_equal, A.mult, ["jm", "pc"], [name])
     ts(T.mk[:], T.jm[:, 0:8], pd, None, A.is_equal, None, ["jm", "pc"], ["mk"])
     ts(T.tie[:], T.jm[:, 0:16], -16.0, 241.0, A.mult, A.add, ["jm"], ["tie"])
-    fill(T.pay[:, 32:48], 0.0, "pay0")
     ts(T.pay[:, 0:16], T.jm[:, 0:16], -16.0, 240.0, A.mult, A.add, ["jm"], ["pay1"])
     ts(T.cut[:], T.jm[:, 0:32], 0.0, -1.0e9, A.is_equal, A.mult, ["jm"], ["cut"])
     fill(T.na[:, 0:1], -1.0, "na0")
     fill(T.VW[:], 0.0, "VW")
     fill(T.NW[:], 0.0, "NW")
+    fill(T.one[0:2, :], 1.0, "one")
+    ts(pc[7], pc[0], -4096.5, 4096.0, A.mult, A.add, ["pc"], ["pc7"])
+    for c in (0, 128):
+        ts(T.cst[0:2, c:c + 128], T.one[0:2, :], T.pc[0:2, 7:8], None, A.mult, None, ["one", "pc7"], ["cst0"])
+    for k, x in ((1, -BIG), (2, BIG)):
+        fill(T.cst[0:1, 256 * k:256 * k + 256], x, "cst%d" % k)
+    ts(T.own[:], T.mk[:], -1.0, 2.0 ** 26, A.add, A.mult, ["mk"], ["own"])
+    ts(T.own[:], T.own[:], pb, None, A.add, None, ["own", "pb"], ["own"])
     ts(T.neye[:], T.jd[:], 0.0, -1.0, A.is_equal, A.mult, ["jd"], ["neye"])
     for name, src in (("eye", "jd"), ("unturn", "jq"), ("turn", "jp")):
         ts(T[name][:], T[src][:], 0.0, None, A.is_equal, None, [src], [name])
-    ts(pc[7], p8, pd, None, A.is_equal, None, ["pc"], ["pc7"])
-    ts(pc[8], ph, -16.0, None, A.add, None, ["pc"], ["pc8"])
-    ts(T.xf[:], T.jm[:, 0:8], 2.0, pc[8], A.mult, A.add, ["jm", "pc8"], ["xf"])
-    ts(T.xo[:], T.xf[:], pc[7], 32.0, A.mult, A.add, ["xf", "pc7"], ["xo"])
-    ts(pc[9], pe, 16.0, -241.0, A.mult, A.add, ["pc"], ["pc9"])
 
     tc(T.tf[0:16, :], T.invi[0:16, :], ["invi"], ["tf"])
     tc(T.invb[0:16, :], T.tf[0:16, :], ["tf"], ["invb"])
     mm(T.m0[:, 0:16], T.invb[0:16, :], T.rep[0:16, 0:16], True, True, ["invb", "rep"], ["m0"])
     mm(T.m1[:, 0:256], T.unturn[:], T.v0[:], True, True, ["unturn", "v0"], ["m1"])
-    tt(T.pay[:, 16:32], T.m0[:, 0:16], T.tie[:], A.add, ["m0", "tie", "pay0", "pay1"], ["pay"])
-    op("v", lambda: V.tensor_reduce(pc[10], T.m0[:, 0:16], AxisListType.X, A.add), ["m0"], ["pc10"])
-    ts(T.ns[:, 0:1], pc[10], -120.0, None, A.add, None, ["pc10"], ["ns0"])
-    ts(T.tgt[:, 0:1], T.ns[:, 0:1], -1.0, pb, A.mult, A.add, ["ns0", "pb"], ["tgt"])
+    tt(T.pay[:, 16:32], T.m0[:, 0:16], T.tie[:], A.add, ["m0", "tie", "pay1"], ["pay"])
+    op("v", lambda: V.tensor_reduce(tot, T.m0[:, 0:16], AxisListType.X, A.add), ["m0"], ["tot"])
+    ts(T.ns[:, 0:1], tot, -120.0, None, A.add, None, ["tot"], ["ns0"])
+    ts(T.pick8[:], T.own[:], T.ns[:, 0:1], None, A.subtract, None, ["ns0", "own"], ["pick8"])
     tc(T.VW[:, 1:257], T.m1[:, 0:256], ["m1"], ["VW"])
-    tc(T.new[:], T.VW[:].indirect(T.tgt[:, 0:1]), ["VW", "tgt"], ["new"])
+    tc(T.wide[:], T.VW[:].indirect(T.pick8[:]), ["VW", "pick8"], ["wide"])
     for name, o, x in (("suph", A.arith_shift_right, 8), ("supl", A.bitwise_and, 255)):
         ts(T.ti[0:16, :], T.supi[0:16, :], x, None, o, None, ["supi"], ["ti"])
-        tc(T.tf[0:16, :], T.ti[0:16, :], ["ti"], ["tf"])
-        tc(T[name][0:16, :], T.tf[0:16, :], ["tf"], [name])
+        ts(T[name][0:16, :], T.ti[0:16, :], 0.0, None, A.add, None, ["ti"], [name])
     for s in range(N):
         ts(T.wl[:, 32 * s:32 * s + 32], T.wx[:], T.mk[:, s:s + 1], None, A.mult, None, ["wx", "mk"], ["wl%d" % s])
     mm(T.m2[:, 0:256], T.rep[:], T.wl[:], True, True, ["rep"] + ["wl%d" % s for s in range(N)], ["m2"])
     for eh in range(2):
         tc(T.wr[:, 128 * eh:128 * eh + 128], T.m2[:, eh:256:2], ["m2"], ["wr%d" % eh])
-    for qh in range(8):
-        ts(T.Wm[:, 256 * qh:256 * qh + 256], T.wr[:], T.mk[:, qh:qh + 1], None, A.mult, None, ["wr0", "wr1", "mk"], ["Wm%d" % qh])
+        ts(T.wn[:, 128 * eh:128 * eh + 128], T.m2[:, eh:256:2], -1.0, None, A.mult, None, ["m2"], ["wn%d" % eh])
 
-    def places(piece, stage):
-        a, b = ((0, 64), (64, 256))[piece]
-        bank = ("ha", "hb")[piece]
-        if stage == 0:
-            tc(T.h1[:, a:b], T[bank][:, 0:b - a], [bank], ["h1%d" % piece])
-        elif stage == 1:
-            ts(T.h2[:, a:b], T.h1[:, a:b], 8191, None, A.bitwise_and, None, ["h1%d" % piece], ["h2%d" % piece])
+    def const(piece, k, start):
+        a, b = PIECES[piece]
+        rows_ = 2 if k == 0 else 1
+        mm(T["x%d" % piece][:, 0:b - a], T.one[0:rows_, :], T.cst[0:rows_, 256 * k:256 * k + b - a], start, False, ["one", "cst%d" % k], ["x%d" % piece])
+
+    def places_ahead():
+        for piece in range(len(PIECES)):
+            const(piece, 0, True)
+
+    def places(piece):
+        a, b = PIECES[piece]
+        bank = "x%d" % piece
+        parts = [(c, d) for c, d in ((a, min(b, 128)), (max(a, 128), b)) if c < d]
+        for name in ("wn", "wr"):
+            for c, d in parts:
+                eh = c // 128
+                mm(T[bank][:, c - a:d - a], T[name][:, 128 * eh:128 * eh + 128], T.wide[:, c % 128:c % 128 + d - c], False,
+                   name == "wr" and d == b, [name + str(eh), "wide"], [bank])
+            if name == "wn":
+                const(piece, 1, False)
+                const(piece, 2, False)
+
+    def offsets(piece):
+        a, b = PIECES[piece]
+        tc(T.off[:, a:b], T["x%d" % piece][:, 0:b - a], ["x%d" % piece], ["off%d" % c for c in range(a // 2, b // 2)])
+
+    def look(q, a, b):
+        out, src = T.G[:, 16 * a:16 * b], T.Y[:].indirect(T.off[:, a:b])
+        reads, writes = Yk + ["off%d" % c for c in range(a // 2, b // 2)], ["G%d" % c for c in range(a // 2, b // 2)]
+        if q == "s":
+            act(out, src, F.Copy, reads, writes)
         else:
-            tc(T.off[:, a:b], T.h2[:, a:b], ["h2%d" % piece], ["off%d" % piece])
+            tc(out, src, reads, writes)
 
     m0c, mcc = T.sc[:, 15:16], T.sc[:, 31:32]
 
@@ -250,9 +275,14 @@ def rank_program(g, core, T, topo):
         elif what == "flags":
             act(na, ns, F.Sign, [kns], [kna])
             act(T.dd[:, 0:1], np_, F.Identity, [knp, kna, kns], ["dd"], bias=ns, scale=na)
-            act(T.sv[:, 0:1], na, F.Identity, [kna, "pc11", "pc12"], ["sv"], bias=pc[12], scale=pc[11])
+        elif what == "pick":
+            ts(T.pick[:, 0:1], mcc, m0c, pb, A.subtract, A.add, ["sc", "pb"], ["pick"])
+        elif what == "new":
+            tc(T.new[:], T.NW[:].indirect(T.pick[:, 0:1]), ["NW", "pick"], ["new"])
+        elif what == "spare":
+            ts(T.sv[:, 0:1], ns, 0.0, gap, A.is_equal, A.mult, [kns, "gap"], ["sv"])
         elif what == "tgt":
-            ts(T.tgt[:, 0:1], T.sv[:, 0:1], ns, None, A.subtract, None, [kns, "sv"], ["tgt"])
+            ts(T.tgt[:, 0:1], T.sv[:, 0:1], ns, pb, A.subtract, A.add, [kns, "sv", "pb"], ["tgt"])
         elif what == "put":
             tc(T.VW[:].indirect(T.tgt[:, 0:1]), T.new[:], ["tgt", "new"], ["VW"])
         elif what == "dl":
@@ -267,60 +297,56 @@ def rank_program(g, core, T, topo):
                                   (slice(0, 256), "eye", slice(2, 258), 2)):
             mm(T.m2[:, out], T[eye][:], T.VW[:, src], st == 0, st == 2, [eye, "VW"], ["m2"])
 
+    places_ahead()
     for t in range(STEPS):
-        for eh in range(2):
-            for qh in range(8):
-                c = 128 * eh + 16 * qh
-                bank, c0 = ("ha", c) if c < 64 else ("hb", c - 64)
-                w = 256 * qh + 128 * eh
-                mm(T[bank][:, c0:c0 + 16], T.Wm[:, w:w + 128], T.new[:], True, True, ["Wm%d" % qh, "new"], [bank])
-        for k in range(3):
-            places(0, k)
-        if t:
-            book(t - 1, "tgt")
-        for k in range(3):
-            places(1, k)
-            if t:
-                book(t - 1, ("put", "dl", "pay")[k])
+        for piece in range(len(PIECES)):
+            places(piece)
+        if t == 0:
+            on_v, on_s, sums = tuple(("u", k) for k in range(len(PIECES))) + FIRST_V, FIRST_S, FIRST_SUMS
+        else:
+            on_v, on_s, sums = ON_V, ON_S, SUMS
+        for x in on_v:
+            if x[0] == "u":
+                offsets(x[1])
+            elif x[0] == "g":
+                look("v", x[1], x[2])
+            else:
+                book(t - 1, x)
+        for a, b in on_s:
+            look("s", a, b)
         mirror()
-        on_s, on_v, sums = LATER if t else FIRST
-        for q, calls in (("s", on_s), ("v", on_v)):
-            for a, b in calls:
-                out, src = T.G[:, 16 * a:16 * b], T.Y[:].indirect(T.off[:, a:b])
-                reads, writes = Yk + ["off%d" % (0 if b <= 64 else 1)], ["G%d" % c for c in range(a // 2, b // 2)]
-                if q == "s":
-                    act(out, src, F.Copy, reads, writes)
-                else:
-                    tc(out, src, reads, writes)
-        act(T.NW[:, 1:257], T.m2[:, 0:256], F.Copy, ["m2"], ["NW"])
+        if t < STEPS - 1:
+            places_ahead()
         mm(T.key[:, 0:32], T.suph[0:16, :], T.Rh[0:16, :], True, False, ["suph", "Rh"], ["key"])
         mm(T.key[:, 0:32], T.supl[0:16, :], T.Rl[0:16, :], False, False, ["supl", "Rl"], ["key"])
-        for a, b in sums:
+        for n, (a, b) in enumerate(sums):
             for e in range(16):
                 mm(T.key[a % 128:a % 128 + b - a, 0:32], T.G[:, 16 * a + e:16 * b:16], T.R[:], False, False,
                    ["G%d" % c for c in range(a // 2, b // 2)] + ["R"], ["key"])
+        act(T.NW[:, 1:257], T.m2[:, 0:256], F.Copy, ["m2"], ["NW"])
         mm(T.key[:, 0:32], T.eye[:], T.pay[:, 0:32], False, True, ["eye", "pay"], ["key"])
         op("v", lambda: V.tensor_tensor_scan(T.sc[:], T.cut[:], T.key[:, 0:32], -1.0e9, A.add, A.max), ["cut", "key"], ["sc"])
         if t < STEPS - 1:
-            ts(T.pick[:, 0:1], mcc, m0c, pb, A.subtract, A.add, ["sc", "pb"], ["pick"])
+            ts(T.pick8[:], T.own[:], mcc, m0c, A.add, A.subtract, ["sc", "own"], ["pick8"])
             book(t, "ns")
+            book(t, "pick")
+            tc(T.wide[:], T.NW[:].indirect(T.pick8[:]), ["NW", "pick8"], ["wide"])
         else:
-            book(t, "ns")
-            ts(T.pick[:, 0:1], mcc, m0c, pb, A.subtract, A.add, ["sc", "pb"], ["pick"])
-        tc(T.new[:], T.NW[:].indirect(T.pick[:, 0:1]), ["NW", "pick"], ["new"])
+            for what in ("ns", "pick", "spare", "new"):
+                book(t, what)
         book(t, "flags")
 
-    for what in ("dl", "tgt", "pay", "put"):
+    for what in ("tgt", "dl", "put"):
         book(STEPS - 1, what)
-    tc(T.ex[:], T.pay[:].indirect(T.xo[:]), ["pay", "xo"], ["ex"])
+    mm(T.m0[0:16, 0:128], T.pay[:, 16:32], T.eye[:], True, False, ["pay", "eye"], ["m0"])
+    mm(T.m0[0:16, 0:128], T.dl[:], T.eye[:], False, True, ["dl"], ["m0"])
     mm(T.m1[:, 0:256], T.turn[:], T.VW[:, 1:257], True, True, ["turn", "VW"], ["m1"])
-    mm(T.m0[:, 0:16], T.ex[:], T.rep[:, 0:16], True, True, ["ex", "rep"], ["m0"])
+    ts(T.nt[0:16, :], T.m0[0:16, 0:128], T.pc[0:16, 5:6], None, A.add, None, ["m0", "untie"], ["nt"])
     act(T.vt[:], T.m1[:, 0:256], F.Copy, ["m1"], ["vt"])
-    ts(T.nt[:], T.m0[:, 0:16], pc[9], None, A.add, None, ["m0", "pc9"], ["nt"])
-    dma("y", T.dn[r], T.nt[:], ["nt"], ["dn_own"])
-    to_all(T.vt[:], T.dv[r], "av", ["vt", "nt"], 0)
+    dma("y", T.dn[r], T.nt[0:16, :], ["nt"], ["dn_own"])
+    to_all(T.vt[:], T.dv[r], "av", ["vt"], 0)
     to_all(T.dn[r], T.dn[r], "an", ["dn_own"], 1)
-    dma("s", T.yv[rows, :], T.vt[:], ["vt", "dn_own"], ["yv_own"])
+    dma("s", T.yv[rows, :], T.vt[:], ["vt"], ["yv_own"])
     if r > 0:
         dma("y", T.yv[0:16 * r, :], T.dv[0:r], ["dv_far"], ["yv_a"])
     if r < N - 1:

@@ -1,32 +1,33 @@
 from concourse.bass import DstId, RemoteDMATransfer
 from concourse.mybir import AluOpType as A, AxisListType, ActivationFunctionType as F
 
-N, STEPS = 8, 5
+N, STEPS, SETS, Q = 8, 5, 2, 64
 VWID, SPARE = 288, 258
 BIG = 1.5 * 2.0 ** 36
-PIECES = ((0, 76), (76, 256))
-ON_V = ("spare", "new", ("u", 0), "tgt", ("u", 1), "put", "dl", ("g", 76, 128), "pay", ("g", 176, 224), ("g", 238, 256))
-ON_S = ((0, 76), (128, 176), (224, 238))
-SUMS = ((0, 128), (128, 224), (224, 256))
-FIRST_V = (("g", 64, 128), ("g", 176, 224), ("g", 240, 256))
-FIRST_S = ((0, 64), (128, 176), (224, 240))
-FIRST_SUMS = SUMS
+PIECES = ((0, 64), (64, 128))
+TURN = (("v", 34, 58), ("s", 0, 34), ("s", 64, 96), "scan", ("v", 58, 64), "ns", "pick4", "*pay", "pick", "na", "*mirror",
+        "spare", "*fixed", ("sum", 0, 64), "wide", ("v", 106, 128), "new", ("s", 96, 106), "places", ("sum", 64, 96), "dd",
+        ("sum", 96, 128), "tgt", "u0", "u1", "*last", "*NW", "ahead", "put", "dl")
+FIRST = (("s", 0, 32), ("v", 32, 64), ("s", 64, 96), ("v", 96, 128), "*fixed", ("sum", 0, 64), ("sum", 64, 128), "*last")
 BF, FP, I32, U16 = "bfloat16", "float32", "int32", "uint16"
 SCRATCH = {"stage": ("dram", [N, 128, 1024], BF), "tl": ("dram", [N, 128, 1024], BF), "ws": ("dram", [N, 128, 4], BF),
-           "wd": ("dram", [N, 128, 4], BF), "dv": ("dram", [N, 128, 256], BF), "dn": ("dram", [N, 128, 16], FP)}
-for _dt, _bufs in ((BF, dict(Y=8192, G=4096, wx=32, wl=256, wr=256, wn=256, wide=128, v0=256, VW=VWID, NW=VWID, invb=128,
-                             suph=128, supl=128, eye=128, neye=128, turn=128, unturn=128, rep=128, R=32, Rh=32, Rl=32,
-                             pay=32, new=16, dl=16, vt=256, one=128, cst=1024)),
-                   (FP, dict(tf=128, jm=128, jd=128, jp=128, jq=128, pc=16, mk=8, cut=32, tie=16, sc=32, sv=8,
+           "wd": ("dram", [N, 128, 4], BF), "dn": ("dram", [N, 128, 16], FP)}
+for _dt, _bufs in ((BF, dict(Y=8192, wx=32, wl=256, wr=256, wn=256, v0=256, invb=128, suph=128, supl=128, eye=128, neye=128,
+                             unturn=128, turn=256, rep=128, R=32, Rh=32, Rl=32, pay=32, dl=16, one=128, cst=384)),
+                   (FP, dict(tf=128, jm=128, jd=128, jp=256, jq=128, pc=16, mk=8, cut=32, tie=16, sc=32, sv=8,
                              ns=8, na=8, dd=8, nt=128, own=8)),
-                   (I32, dict(invi=128, supi=128, ti=128, pi=8)),
-                   (U16, dict(off=256, pick=2, tgt=2, pick8=8))):
+                   (I32, dict(invi=128, supi=128, ti=128, pi=8))):
     for _name, _cols in _bufs.items():
         SCRATCH[_name] = ("sbuf", [128, _cols], _dt)
-PSUM = ("x0", "x1", "x2", "x3", "key", "m0", "m1", "m2")
+for _h in range(SETS):
+    SCRATCH["dv%d" % _h] = ("dram", [N, 128, 128], BF)
+    for _dt, _bufs in ((BF, dict(G=32 * Q, VW=VWID, NW=VWID, wide=Q, new=16, vt=128)), (U16, dict(off=2 * Q, pick=2, tgt=2, pick4=4))):
+        for _name, _cols in _bufs.items():
+            SCRATCH[_name + str(_h)] = ("sbuf", [128, _cols], _dt)
+PSUM = ("x0", "x1", "key0", "key1", "m0", "m1", "m2")
 for _name in PSUM:
     SCRATCH[_name] = ("psum", [128, 512], FP)
-SEMAPHORES = (["cg", "cv", "cs", "ct", "sent", "aw", "av", "an"] + ["at%d" % s for s in range(N)]
+SEMAPHORES = (["cg", "cv", "cs", "ct", "sent", "aw", "av0", "av1", "an"] + ["at%d" % s for s in range(N)]
               + ["d%d" % k for k in range(32)])
 
 
@@ -34,6 +35,7 @@ def make_sched(g, T):
     queue = {"g": g, "v": g.vector, "s": g.scalar, "t": g.tensor, "y": g.sync}
     counter = {"g": "cg", "v": "cv", "s": "cs", "t": "ct"}
     total, known, writer, readers, ndma = {}, {q: {} for q in queue}, {}, {}, [0]
+    held = []
 
     def order(q, reads, writes):
         toks = []
@@ -63,9 +65,16 @@ def make_sched(g, T):
         for k in writes:
             writer[k] = tok; readers[k] = []
 
-    def op(q, call, reads, writes):
+    def op(q, call, reads, writes, more=False):
         order(q, reads, writes)
+        if more:
+            call()
+            held.append((reads, writes))
+            return
         call().then_inc(T.sem[counter[q]], 1)
+        for rd, wr in held:
+            reads, writes = reads + rd, writes + wr
+        del held[:]
         done(q, counter[q], 1, reads, writes, q)
 
     def dma(q, out, in_, reads, writes):
@@ -136,18 +145,23 @@ def rank_program(g, core, T, topo):
     def act(out, in_, f, reads, writes, **kw):
         op("s", lambda: S.activation(out, in_, f, **kw), reads, writes)
 
-    def mm(out, lhsT, rhs, start, stop, reads, writes):
-        op("t", lambda: P.matmul(out, lhsT, rhs, start, stop), reads, writes)
+    def mm(out, lhsT, rhs, start, stop, reads, writes, more=False):
+        op("t", lambda: P.matmul(out, lhsT, rhs, start, stop), reads, writes, more)
 
     def iota(name, pattern, cm):
         op("g", lambda: g.iota(T[name][:], pattern, 0, cm, allow_small_or_imprecise_dtypes=True), [], [name])
 
+    def B(name, h):
+        return T[name + str(h)]
+
     rows = slice(16 * r, 16 * r + 16)
+    part = [slice(Q * h, Q * h + Q) for h in range(SETS)]
     order_to = [x for k in range(len(far)) for x in ([far_to[k]] + near_to[k:k + 1])]
     pair = len(eng) // N
     lands("wd_far", "aw", (N - 1) * pair)
-    lands("dv_far", "av", (N - 1) * E)
     lands("dn_far", "an", (N - 1) * E)
+    for h in range(SETS):
+        lands("dv_far%d" % h, "av%d" % h, (N - 1) * E)
     for s in order_to:
         lands("tl%d" % s, "at%d" % s, E)
 
@@ -163,7 +177,6 @@ def rank_program(g, core, T, topo):
     iota("jm", [[0, 8], [1, 16]], 0)
     iota("jd", [[-1, 128]], 1)
     iota("jq", [[1, 8], [8, 16]], -1)
-    iota("jp", [[1, 16], [16, 8]], -1)
     wts = [RemoteDMATransfer(dst_ids=[dst(s)], dma_engine_mask=sum(1 << e for e in eng[pair * k:pair * k + pair]),
                              remote_sem=T.sem.aw, srcs=[T.ws[s]], dsts=[T.wd[r]]) for k, s in enumerate(order_to)]
     remote(lambda: g.remote_dma_fused(wts, local_sem=T.sem.sent), (N - 1) * pair, ["ws"])
@@ -171,6 +184,9 @@ def rank_program(g, core, T, topo):
         rid, pid, _ = topo.addr(cores[s])
         m = mask[0 if s in far else 1]
         remote(lambda: g.remote_dma(T.tl[r], T.stage[s], T.sem["at%d" % r], T.sem.sent, pid, rid, m), E, ["stage%d" % s])
+    for k in range(2):
+        op("g", lambda: g.iota(T.jp[:, 128 * k:128 * k + 128], [[1, 16], [16, 4], [128 - 256 * k, 2]], 128 * k, 0,
+                               allow_small_or_imprecise_dtypes=True), [], ["jp%d" % k])
 
     dma("s", T.wx[:], T.wd[:], ["wd_own", "wd_far"], ["wx"])
     for k, s in enumerate(near_from):
@@ -183,12 +199,14 @@ def rank_program(g, core, T, topo):
 
     ts(T.pi[:, 1:2], T.pi[:, 0:1], 15, None, A.bitwise_and, None, ["pi0"], ["pi1"])
     ts(T.pi[:, 2:3], T.pi[:, 0:1], 4, None, A.arith_shift_right, None, ["pi0"], ["pi2"])
-    tc(T.pc[:, 0:3], T.pi[:, 0:3], ["pi%d" % k for k in range(3)], ["pc"])
+    ts(T.pi[:, 3:4], T.pi[:, 0:1], Q - 1, None, A.bitwise_and, None, ["pi0"], ["pi3"])
+    tc(T.pc[:, 0:4], T.pi[:, 0:4], ["pi%d" % k for k in range(4)], ["pc"])
     pc = [T.pc[:, k:k + 1] for k in range(16)]
-    pm, pd, pb, gap, untie, tot = pc[1:7]
+    pm, pd, pq, pb, gap, tot = pc[1:7]
+    PB, GAP, UNTIE, HALF = 4, 5, 8, 7
     ts(pb, pm, 16.0, None, A.mult, None, ["pc"], ["pb"])
     ts(gap, pm, -15.0, float(SPARE), A.mult, A.add, ["pc"], ["gap"])
-    ts(untie, pm, 16.0, -241.0, A.mult, A.add, ["pc"], ["untie"])
+    ts(pc[UNTIE], pm, 16.0, -241.0, A.mult, A.add, ["pc"], ["untie"])
     ts(T.rep[:], T.jm[:], pm, None, A.is_equal, None, ["jm", "pc"], ["rep"])
     for name, x in (("R", 256.0), ("Rh", -65536.0), ("Rl", -256.0)):
         ts(T[name][:], T.jm[:, 0:32], pm, x, A.is_equal, A.mult, ["jm", "pc"], [name])
@@ -196,31 +214,33 @@ def rank_program(g, core, T, topo):
     ts(T.tie[:], T.jm[:, 0:16], -16.0, 241.0, A.mult, A.add, ["jm"], ["tie"])
     ts(T.pay[:, 0:16], T.jm[:, 0:16], -16.0, 240.0, A.mult, A.add, ["jm"], ["pay1"])
     ts(T.cut[:], T.jm[:, 0:32], 0.0, -1.0e9, A.is_equal, A.mult, ["jm"], ["cut"])
-    fill(T.na[:, 0:1], -1.0, "na0")
-    fill(T.VW[:], 0.0, "VW")
-    fill(T.NW[:], 0.0, "NW")
+    fill(T.na[:, 0:1], -1.0, "na")
+    for h in range(SETS):
+        for name in ("VW", "NW", "pick", "pick4"):
+            fill(B(name, h)[:], 0, name + str(h))
+        ts(B("tgt", h)[:, 0:1], pm, float(SPARE), None, A.add, None, ["pc"], ["tgt%d" % h])
     fill(T.one[0:2, :], 1.0, "one")
-    ts(pc[7], pc[0], -4096.5, 4096.0, A.mult, A.add, ["pc"], ["pc7"])
-    for c in (0, 128):
-        ts(T.cst[0:2, c:c + 128], T.one[0:2, :], T.pc[0:2, 7:8], None, A.mult, None, ["one", "pc7"], ["cst0"])
+    ts(pc[HALF], pc[0], -4096.5, 4096.0, A.mult, A.add, ["pc"], ["half"])
+    ts(T.cst[0:2, 0:128], T.one[0:2, :], T.pc[0:2, HALF:HALF + 1], None, A.mult, None, ["one", "half"], ["cst0"])
     for k, x in ((1, -BIG), (2, BIG)):
-        fill(T.cst[0:1, 256 * k:256 * k + 256], x, "cst%d" % k)
+        fill(T.cst[0:1, 128 * k:128 * k + 128], x, "cst%d" % k)
     ts(T.own[:], T.mk[:], -1.0, 2.0 ** 26, A.add, A.mult, ["mk"], ["own"])
     ts(T.own[:], T.own[:], pb, None, A.add, None, ["own", "pb"], ["own"])
     ts(T.neye[:], T.jd[:], 0.0, -1.0, A.is_equal, A.mult, ["jd"], ["neye"])
-    for name, src in (("eye", "jd"), ("unturn", "jq"), ("turn", "jp")):
+    for name, src in (("eye", "jd"), ("unturn", "jq")):
         ts(T[name][:], T[src][:], 0.0, None, A.is_equal, None, [src], [name])
 
     tc(T.tf[0:16, :], T.invi[0:16, :], ["invi"], ["tf"])
     tc(T.invb[0:16, :], T.tf[0:16, :], ["tf"], ["invb"])
     mm(T.m0[:, 0:16], T.invb[0:16, :], T.rep[0:16, 0:16], True, True, ["invb", "rep"], ["m0"])
     mm(T.m1[:, 0:256], T.unturn[:], T.v0[:], True, True, ["unturn", "v0"], ["m1"])
-    tt(T.pay[:, 16:32], T.m0[:, 0:16], T.tie[:], A.add, ["m0", "tie", "pay1"], ["pay"])
+    tt(T.pay[:, 16:32], T.m0[:, 0:16], T.tie[:], A.add, ["m0", "tie", "pay1"], ["pay0", "pay1"])
     op("v", lambda: V.tensor_reduce(tot, T.m0[:, 0:16], AxisListType.X, A.add), ["m0"], ["tot"])
-    ts(T.ns[:, 0:1], tot, -120.0, None, A.add, None, ["tot"], ["ns0"])
-    ts(T.pick8[:], T.own[:], T.ns[:, 0:1], None, A.subtract, None, ["ns0", "own"], ["pick8"])
-    tc(T.VW[:, 1:257], T.m1[:, 0:256], ["m1"], ["VW"])
-    tc(T.wide[:], T.VW[:].indirect(T.pick8[:]), ["VW", "pick8"], ["wide"])
+    ts(T.ns[:, 0:1], tot, -120.0, None, A.add, None, ["tot"], ["ns0_0", "ns1_0"])
+    for h in range(SETS):
+        ts(B("pick4", h)[part[h], :], T.own[part[h], 4 * h:4 * h + 4], T.ns[part[h], 0:1], None, A.subtract, None, ["ns0_0", "own"], ["pick4%d" % h])
+        tc(B("VW", h)[part[h], 1:257], T.m1[part[h], 0:256], ["m1"], ["VW%d" % h])
+        tc(B("wide", h)[:], B("VW", h)[:].indirect(B("pick4", h)[:]), ["VW%d" % h, "pick4%d" % h], ["wide%d" % h])
     for name, o, x in (("suph", A.arith_shift_right, 8), ("supl", A.bitwise_and, 255)):
         ts(T.ti[0:16, :], T.supi[0:16, :], x, None, o, None, ["supi"], ["ti"])
         ts(T[name][0:16, :], T.ti[0:16, :], 0.0, None, A.add, None, ["ti"], [name])
@@ -230,126 +250,142 @@ def rank_program(g, core, T, topo):
     for eh in range(2):
         tc(T.wr[:, 128 * eh:128 * eh + 128], T.m2[:, eh:256:2], ["m2"], ["wr%d" % eh])
         ts(T.wn[:, 128 * eh:128 * eh + 128], T.m2[:, eh:256:2], -1.0, None, A.mult, None, ["m2"], ["wn%d" % eh])
+    ts(T.turn[:], T.jp[:], pq, None, A.is_equal, None, ["jp0", "jp1", "pc"], ["turn"])
 
-    def const(piece, k, start):
+    def const(piece, k, more):
         a, b = PIECES[piece]
-        rows_ = 2 if k == 0 else 1
-        mm(T["x%d" % piece][:, 0:b - a], T.one[0:rows_, :], T.cst[0:rows_, 256 * k:256 * k + b - a], start, False, ["one", "cst%d" % k], ["x%d" % piece])
+        n = 2 if k == 0 else 1
+        mm(T["x%d" % piece][:, 0:b - a], T.one[0:n, :], T.cst[0:n, 128 * k:128 * k + b - a], k == 0, False,
+           ["one", "cst%d" % k], ["x%d" % piece], more)
 
-    def places_ahead():
-        for piece in range(len(PIECES)):
-            const(piece, 0, True)
-
-    def places(piece):
+    def places(h, piece):
         a, b = PIECES[piece]
         bank = "x%d" % piece
-        parts = [(c, d) for c, d in ((a, min(b, 128)), (max(a, 128), b)) if c < d]
+        parts = [(c, d) for c, d in ((a, min(b, Q)), (max(a, Q), b)) if c < d]
         for name in ("wn", "wr"):
             for c, d in parts:
-                eh = c // 128
-                mm(T[bank][:, c - a:d - a], T[name][:, 128 * eh:128 * eh + 128], T.wide[:, c % 128:c % 128 + d - c], False,
-                   name == "wr" and d == b, [name + str(eh), "wide"], [bank])
+                eh, last = c // Q, name == "wr" and d == b
+                mm(T[bank][:, c - a:d - a], T[name][:, 128 * eh:128 * eh + 128], B("wide", h)[:, c % Q:c % Q + d - c], False,
+                   last, [name + str(eh), "wide%d" % h], [bank], not last)
             if name == "wn":
-                const(piece, 1, False)
-                const(piece, 2, False)
+                const(piece, 1, True)
+                const(piece, 2, True)
 
-    def offsets(piece):
-        a, b = PIECES[piece]
-        tc(T.off[:, a:b], T["x%d" % piece][:, 0:b - a], ["x%d" % piece], ["off%d" % c for c in range(a // 2, b // 2)])
+    def cols(name, h, a, b):
+        return ["%s%d_%d" % (name, h, c) for c in range(a // 2, b // 2)]
 
-    def look(q, a, b):
-        out, src = T.G[:, 16 * a:16 * b], T.Y[:].indirect(T.off[:, a:b])
-        reads, writes = Yk + ["off%d" % c for c in range(a // 2, b // 2)], ["G%d" % c for c in range(a // 2, b // 2)]
+    def look(h, q, a, b):
+        out, src = B("G", h)[:, 16 * a:16 * b], T.Y[:].indirect(B("off", h)[:, a:b])
+        reads, writes = Yk + cols("off", h, a, b), cols("G", h, a, b)
         if q == "s":
             act(out, src, F.Copy, reads, writes)
         else:
             tc(out, src, reads, writes)
 
-    m0c, mcc = T.sc[:, 15:16], T.sc[:, 31:32]
+    def sums(h, a, b):
+        p = Q * h + a % Q
+        for e in range(16):
+            mm(B("key", h)[p:p + b - a, 0:32], B("G", h)[:, 16 * a + e:16 * b:16], T.R[:], False, False,
+               cols("G", h, a, b) + ["R"], ["key%d" % h], e < 15)
 
-    def book(t, what):
-        ns, np_, na, nap = T.ns[:, t + 1:t + 2], T.ns[:, t:t + 1], T.na[:, t + 1:t + 2], T.na[:, t:t + 1]
-        kns, knp, kna, knap = "ns%d" % (t + 1), "ns%d" % t, "na%d" % (t + 1), "na%d" % t
-        if what == "ns":
-            ts(ns, mcc, m0c, nap, A.subtract, A.mult, ["sc", knap], [kns])
-        elif what == "flags":
+    def call(h, t, what):
+        H, p = str(h), part[h]
+        key, VW, NW = B("key", h), B("VW", h), B("NW", h)
+        ns, np_, na, nap = T.ns[p, t + 1:t + 2], T.ns[p, t:t + 1], T.na[p, t + 1:t + 2], T.na[p, t:t + 1]
+        kns, knp = "ns%d_%d" % (h, t + 1), "ns%d_%d" % (h, t)
+        kna, knap = "na%d_%d" % (h, t + 1), "na%d_%d" % (h, t) if t else "na"
+        m0c, mcc, base = T.sc[p, 15:16], T.sc[p, 31:32], T.pc[p, PB:PB + 1]
+        if what == "fixed":
+            mm(key[p, 0:32], T.suph[0:16, p], T.Rh[0:16, :], True, False, ["suph", "Rh"], ["key" + H], True)
+            mm(key[p, 0:32], T.supl[0:16, p], T.Rl[0:16, :], False, False, ["supl", "Rl"], ["key" + H])
+        elif what == "last":
+            mm(key[p, 0:32], T.eye[p, p], T.pay[p, 0:32], False, True, ["eye", "pay" + H], ["key" + H])
+        elif what == "scan":
+            op("v", lambda: V.tensor_tensor_scan(T.sc[p, :], T.cut[p, :], key[p, 0:32], -1.0e9, A.add, A.max), ["cut", "key" + H], ["sc" + H])
+        elif what == "pick4":
+            ts(B("pick4", h)[p, :], T.own[p, 4 * h:4 * h + 4], mcc, m0c, A.add, A.subtract, ["sc" + H, "own"], ["pick4" + H])
+        elif what == "wide":
+            tc(B("wide", h)[:], NW[:].indirect(B("pick4", h)[:]), ["NW" + H, "pick4" + H], ["wide" + H])
+        elif what == "ahead":
+            for piece in range(len(PIECES)):
+                const(piece, 0, False)
+        elif what == "places":
+            for piece in range(len(PIECES)):
+                places(h, piece)
+        elif what in ("u0", "u1"):
+            a, b = PIECES[int(what[1])]
+            tc(B("off", h)[:, a:b], T["x" + what[1]][:, 0:b - a], ["x" + what[1]], cols("off", h, a, b))
+        elif what == "ns":
+            ts(ns, mcc, m0c, nap, A.subtract, A.mult, ["sc" + H, knap], [kns])
+        elif what == "na":
             act(na, ns, F.Sign, [kns], [kna])
-            act(T.dd[:, 0:1], np_, F.Identity, [knp, kna, kns], ["dd"], bias=ns, scale=na)
+        elif what == "dd":
+            act(T.dd[p, 0:1], np_, F.Identity, [knp, kna, kns], ["dd" + H], bias=ns, scale=na)
         elif what == "pick":
-            ts(T.pick[:, 0:1], mcc, m0c, pb, A.subtract, A.add, ["sc", "pb"], ["pick"])
+            ts(B("pick", h)[p, 0:1], mcc, m0c, base, A.subtract, A.add, ["sc" + H, "pb"], ["pick" + H])
         elif what == "new":
-            tc(T.new[:], T.NW[:].indirect(T.pick[:, 0:1]), ["NW", "pick"], ["new"])
+            tc(B("new", h)[:], NW[:].indirect(B("pick", h)[:, 0:1]), ["NW" + H, "pick" + H], ["new" + H])
         elif what == "spare":
-            ts(T.sv[:, 0:1], ns, 0.0, gap, A.is_equal, A.mult, [kns, "gap"], ["sv"])
+            ts(T.sv[p, 0:1], ns, 0.0, T.pc[p, GAP:GAP + 1], A.is_equal, A.mult, [kns, "gap"], ["sv" + H])
         elif what == "tgt":
-            ts(T.tgt[:, 0:1], T.sv[:, 0:1], ns, pb, A.subtract, A.add, [kns, "sv", "pb"], ["tgt"])
+            ts(B("tgt", h)[p, 0:1], T.sv[p, 0:1], ns, base, A.subtract, A.add, [kns, "sv" + H, "pb"], ["tgt" + H])
         elif what == "put":
-            tc(T.VW[:].indirect(T.tgt[:, 0:1]), T.new[:], ["tgt", "new"], ["VW"])
+            tc(VW[:].indirect(B("tgt", h)[:, 0:1]), B("new", h)[:], ["tgt" + H, "new" + H], ["VW" + H])
         elif what == "dl":
-            ts(T.dl[:], T.key[:, 0:16], m0c, T.dd[:, 0:1], A.is_equal, A.mult, ["key", "sc", "dd"], ["dl"])
-        else:
-            tt(T.pay[:, 16:32], T.pay[:, 16:32], T.dl[:], A.add, ["pay", "dl"], ["pay"])
+            ts(T.dl[p, :], key[p, 0:16], m0c, T.dd[p, 0:1], A.is_equal, A.mult, ["key" + H, "sc" + H, "dd" + H], ["dl" + H])
+        elif what == "pay":
+            tt(T.pay[p, 16:32], T.pay[p, 16:32], T.dl[p, :], A.add, ["pay" + H, "dl" + H], ["pay" + H])
+        elif what == "mirror":
+            for out, eye, src, st in ((slice(0, 256), "neye", slice(1, 257), 0), (slice(0, 256, 16), "eye", slice(16, 257, 16), 1),
+                                      (slice(0, 256, 16), "neye", slice(0, 256, 16), 1), (slice(15, 256, 16), "eye", slice(1, 257, 16), 1),
+                                      (slice(15, 256, 16), "neye", slice(17, 258, 16), 1), (slice(0, 256), "eye", slice(0, 256), 1),
+                                      (slice(0, 256), "eye", slice(2, 258), 2)):
+                mm(T.m2[p, out], T[eye][p, p], VW[p, src], st == 0, st == 2, [eye, "VW" + H], ["m2"], st < 2)
+        elif what == "NW":
+            act(NW[p, 1:257], T.m2[p, 0:256], F.Copy, ["m2"], ["NW" + H])
+        elif what == "out":
+            for k in range(2):
+                mm(T.m1[:, 0:128], T.turn[p, 128 * k:128 * k + 128], VW[p, 1 + 128 * k:129 + 128 * k], k == 0, k == 1, ["turn", "VW" + H], ["m1"], k == 0)
+            act(B("vt", h)[:], T.m1[:, 0:128], F.Copy, ["m1"], ["vt" + H])
+            to_all(B("vt", h)[:], B("dv", h)[r], "av" + H, ["vt" + H], 0)
+        elif what == "store":
+            c = slice(1024 * h, 1024 * h + 1024)
+            dma("s", T.yv[rows, c], B("vt", h)[:], ["vt" + H], ["yv_own" + H])
+            if r > 0:
+                dma("y", T.yv[0:16 * r, c], B("dv", h)[0:r], ["dv_far" + H], ["yv_a" + H])
+            if r < N - 1:
+                dma("y", T.yv[16 * r + 16:128, c], B("dv", h)[r + 1:N], ["dv_far" + H], ["yv_b" + H])
+        elif what == "slots":
+            mm(T.m0[0:16, 0:128], T.pay[:, 16:32], T.eye[:], True, False, ["pay0", "pay1", "eye"], ["m0"], True)
+            mm(T.m0[0:16, 0:128], T.dl[:], T.eye[:], False, True, ["dl0", "dl1"], ["m0"])
+            ts(T.nt[0:16, :], T.m0[0:16, 0:128], T.pc[0:16, UNTIE:UNTIE + 1], None, A.add, None, ["m0", "untie"], ["nt"])
+            dma("y", T.dn[r], T.nt[0:16, :], ["nt"], ["dn_own"])
 
-    def mirror():
-        for out, eye, src, st in ((slice(0, 256), "neye", slice(1, 257), 0), (slice(0, 256, 16), "eye", slice(16, 257, 16), 1),
-                                  (slice(0, 256, 16), "neye", slice(0, 256, 16), 1), (slice(15, 256, 16), "eye", slice(1, 257, 16), 1),
-                                  (slice(15, 256, 16), "neye", slice(17, 258, 16), 1), (slice(0, 256), "eye", slice(0, 256), 1),
-                                  (slice(0, 256), "eye", slice(2, 258), 2)):
-            mm(T.m2[:, out], T[eye][:], T.VW[:, src], st == 0, st == 2, [eye, "VW"], ["m2"])
-
-    places_ahead()
-    for t in range(STEPS):
-        for piece in range(len(PIECES)):
-            places(piece)
-        if t == 0:
-            on_v, on_s, sums = tuple(("u", k) for k in range(len(PIECES))) + FIRST_V, FIRST_S, FIRST_SUMS
-        else:
-            on_v, on_s, sums = ON_V, ON_S, SUMS
-        for x in on_v:
-            if x[0] == "u":
-                offsets(x[1])
-            elif x[0] == "g":
-                look("v", x[1], x[2])
-            else:
-                book(t - 1, x)
-        for a, b in on_s:
-            look("s", a, b)
-        mirror()
-        if t < STEPS - 1:
-            places_ahead()
-        mm(T.key[:, 0:32], T.suph[0:16, :], T.Rh[0:16, :], True, False, ["suph", "Rh"], ["key"])
-        mm(T.key[:, 0:32], T.supl[0:16, :], T.Rl[0:16, :], False, False, ["supl", "Rl"], ["key"])
-        for n, (a, b) in enumerate(sums):
-            for e in range(16):
-                mm(T.key[a % 128:a % 128 + b - a, 0:32], T.G[:, 16 * a + e:16 * b:16], T.R[:], False, False,
-                   ["G%d" % c for c in range(a // 2, b // 2)] + ["R"], ["key"])
-        act(T.NW[:, 1:257], T.m2[:, 0:256], F.Copy, ["m2"], ["NW"])
-        mm(T.key[:, 0:32], T.eye[:], T.pay[:, 0:32], False, True, ["eye", "pay"], ["key"])
-        op("v", lambda: V.tensor_tensor_scan(T.sc[:], T.cut[:], T.key[:, 0:32], -1.0e9, A.add, A.max), ["cut", "key"], ["sc"])
-        if t < STEPS - 1:
-            ts(T.pick8[:], T.own[:], mcc, m0c, A.add, A.subtract, ["sc", "own"], ["pick8"])
-            book(t, "ns")
-            book(t, "pick")
-            tc(T.wide[:], T.NW[:].indirect(T.pick8[:]), ["NW", "pick8"], ["wide"])
-        else:
-            for what in ("ns", "pick", "spare", "new"):
-                book(t, what)
-        book(t, "flags")
-
-    for what in ("tgt", "dl", "put"):
-        book(STEPS - 1, what)
-    mm(T.m0[0:16, 0:128], T.pay[:, 16:32], T.eye[:], True, False, ["pay", "eye"], ["m0"])
-    mm(T.m0[0:16, 0:128], T.dl[:], T.eye[:], False, True, ["dl"], ["m0"])
-    mm(T.m1[:, 0:256], T.turn[:], T.VW[:, 1:257], True, True, ["turn", "VW"], ["m1"])
-    ts(T.nt[0:16, :], T.m0[0:16, 0:128], T.pc[0:16, 5:6], None, A.add, None, ["m0", "untie"], ["nt"])
-    act(T.vt[:], T.m1[:, 0:256], F.Copy, ["m1"], ["vt"])
-    dma("y", T.dn[r], T.nt[0:16, :], ["nt"], ["dn_own"])
-    to_all(T.vt[:], T.dv[r], "av", ["vt"], 0)
+    for h in range(SETS):
+        for what in ("ahead", "places", "u0", "u1", "mirror", "NW"):
+            call(h, 0, what)
+    call(0, 0, "ahead")
+    turns = [(h, t) for t in range(STEPS) for h in range(SETS)]
+    for n, (h, t) in enumerate(turns):
+        for x in TURN if n else FIRST:
+            if x[0] == "sum":
+                sums(h, x[1], x[2])
+            elif isinstance(x, tuple):
+                look(h, x[0], x[1], x[2])
+            elif x[0] == "*":
+                if t or x in ("*fixed", "*last"):
+                    call(h, t - (x not in ("*fixed", "*last")), x[1:])
+            elif n < len(turns) - 1 or x not in ("pick4", "wide", "places", "u0", "u1", "mirror", "NW", "ahead", "pay"):
+                if n < len(turns) - 2 or x != "ahead":
+                    call(turns[n - 1][0], turns[n - 1][1], x)
+    for x in TURN:
+        if x in ("*na", "*dd", "*spare", "*new", "*tgt", "*dl", "*put"):
+            call(0, STEPS - 1, x[1:])
+    call(0, STEPS - 1, "out")
+    for what in ("scan", "ns", "pick", "spare", "na", "dd", "new", "tgt", "dl", "put", "slots", "out"):
+        call(1, STEPS - 1, what)
     to_all(T.dn[r], T.dn[r], "an", ["dn_own"], 1)
-    dma("s", T.yv[rows, :], T.vt[:], ["vt"], ["yv_own"])
-    if r > 0:
-        dma("y", T.yv[0:16 * r, :], T.dv[0:r], ["dv_far"], ["yv_a"])
-    if r < N - 1:
-        dma("s" if r > 0 else "y", T.yv[16 * r + 16:128, :], T.dv[r + 1:N], ["dv_far"], ["yv_b"])
-    dma("y" if 0 < r < N - 1 else "s", T.yi[:], T.dn[:], ["dn_own", "dn_far"], ["yi"])
+    for h in range(SETS):
+        call(h, STEPS - 1, "store")
+    dma("s", T.yi[:], T.dn[:], ["dn_own", "dn_far"], ["yi"])
     finish()

@@ -4,30 +4,39 @@ from concourse.mybir import AluOpType as A, AxisListType, ActivationFunctionType
 N, STEPS, SETS, Q = 8, 5, 2, 64
 VWID, SPARE = 288, 258
 BIG = 1.5 * 2.0 ** 36
+PLAIN = 20
+CHUNKS = (13, 20, 12)
+SHARE = (4, 6)
+WAIT, SLACK, FIRST_CALL = 0.22, 0.1, 1.8
 PIECES = ((0, 64), (64, 128))
-TURN = (("v", 34, 58), ("s", 0, 34), ("s", 64, 96), "scan", ("v", 58, 64), "ns", "pick4", "*pay", "pick", "na", "*mirror",
-        "spare", "*fixed", ("sum", 0, 64), "wide", ("v", 106, 128), "new", ("s", 96, 106), "places", ("sum", 64, 96), "dd",
-        ("sum", 96, 128), "tgt", "u0", "u1", "*last", "*NW", "ahead", "put", "dl")
-FIRST = (("s", 0, 32), ("v", 32, 64), ("s", 64, 96), ("v", 96, 128), "*fixed", ("sum", 0, 64), ("sum", 64, 128), "*last")
+TURN = (("s", 0, 36), "*fixed", "*mirror", ("v", 36, 58), "scan", ("v", 58, 64), ("s", 64, 94), "pick4", "ns", "pick", "wide",
+        ("sum", 0, 64), "spare", "places", "na", ("s", 94, 104), ("v", 104, 128), "dd", "new", ("sum", 64, 96), "*NW", "tgt",
+        "u0", "dl", ("sum", 96, 128), "u1", "put", "ahead", "pay")
+LAST = (("v", 32, 56), ("s", 0, 32), ("s", 64, 96), "scan", ("v", 56, 64), "ns", "pick", "*fixed", "*mirror",
+        ("sum", 0, 64), ("v", 102, 116), "spare", "new", "moved", ("s", 96, 102), ("v", 116, 128), "tgt", "dla", "dlb", ("sum", 64, 96),
+        "put", ("sum", 96, 128), "*NW", "out", "own", "slots")
+END = ("scan", "ns", "pick", "spare", "new", "moved", "dla", "tgt", "dlb", "put", "slots", "out", "nt")
+FIRST = (("s", 0, 32), ("v", 32, 64), ("s", 64, 96), ("v", 96, 128), "*fixed", ("sum", 0, 64), ("sum", 64, 128))
 BF, FP, I32, U16 = "bfloat16", "float32", "int32", "uint16"
-SCRATCH = {"stage": ("dram", [N, 128, 1024], BF), "tl": ("dram", [N, 128, 1024], BF), "ws": ("dram", [N, 128, 4], BF),
-           "wd": ("dram", [N, 128, 4], BF), "dn": ("dram", [N, 128, 16], FP)}
-for _dt, _bufs in ((BF, dict(Y=8192, wx=32, wl=256, wr=256, wn=256, v0=256, invb=128, suph=128, supl=128, eye=128, neye=128,
-                             unturn=128, turn=256, rep=128, R=32, Rh=32, Rl=32, pay=32, dl=16, one=128, cst=384)),
-                   (FP, dict(tf=128, jm=128, jd=128, jp=256, jq=128, pc=16, mk=8, cut=32, tie=16, sc=32, sv=8,
+SCRATCH = {"dn": ("dram", [N, 128, 16], FP), "stage": ("dram", [N, 128, 16 * PLAIN], BF), "tl": ("dram", [N, 128, 16 * PLAIN], BF)}
+for _dt, _bufs in ((BF, dict(mine=8320, Z=8320, X=8320, Y=8320, wl=256, wr=256, v0=256, invb=128, suph=128, supl=128,
+                             eye=128, neye=128, unturn=128, turn=256, rep=128, R=32, sel=512, dl=16, dm=16, one=128, cst=256,
+                             jm=128, jd=128, jp=256, jq=128)),
+                   (FP, dict(tf=128, pc=16, mk=8, cut=32, tie=16, sc=32, sv=8,
                              ns=8, na=8, dd=8, nt=128, own=8)),
-                   (I32, dict(invi=128, supi=128, ti=128, pi=8))):
+                   (I32, dict(invi=128, supi=128, ti=128, tj=128, pi=8))):
     for _name, _cols in _bufs.items():
         SCRATCH[_name] = ("sbuf", [128, _cols], _dt)
 for _h in range(SETS):
     SCRATCH["dv%d" % _h] = ("dram", [N, 128, 128], BF)
-    for _dt, _bufs in ((BF, dict(G=32 * Q, VW=VWID, NW=VWID, wide=Q, new=16, vt=128)), (U16, dict(off=2 * Q, pick=2, tgt=2, pick4=4))):
+    for _dt, _bufs in ((BF, dict(G=32 * Q, VW=VWID, NW=VWID, wide=Q, new=16, vt=128, wn=256, fix=Q, pay=32)),
+                       (U16, dict(off=2 * Q, pick=2, tgt=2, pick4=4))):
         for _name, _cols in _bufs.items():
             SCRATCH[_name + str(_h)] = ("sbuf", [128, _cols], _dt)
-PSUM = ("x0", "x1", "key0", "key1", "m0", "m1", "m2")
+PSUM = ("x0", "x1", "key0", "key1", "m2", "tb0", "tb1", "tb2")
 for _name in PSUM:
-    SCRATCH[_name] = ("psum", [128, 512], FP)
-SEMAPHORES = (["cg", "cv", "cs", "ct", "sent", "aw", "av0", "av1", "an"] + ["at%d" % s for s in range(N)]
+    SCRATCH[_name] = ("psum", [128, 1024], BF) if _name[0] == "t" else ("psum", [128, 512], FP)
+SEMAPHORES = (["cg", "cv", "cs", "ct", "sent", "av0", "av1", "an"] + ["ac%d" % c for c in range(8)]
               + ["d%d" % k for k in range(32)])
 
 
@@ -35,7 +44,7 @@ def make_sched(g, T):
     queue = {"g": g, "v": g.vector, "s": g.scalar, "t": g.tensor, "y": g.sync}
     counter = {"g": "cg", "v": "cv", "s": "cs", "t": "ct"}
     total, known, writer, readers, ndma = {}, {q: {} for q in queue}, {}, {}, [0]
-    held = []
+    held = {q: [] for q in queue}
 
     def order(q, reads, writes):
         toks = []
@@ -48,13 +57,13 @@ def make_sched(g, T):
             if k in writer:
                 toks.append(writer[k])
             toks += readers.get(k, [])
-        toks = [tok for tok in toks if not (q == "t" and tok[3] == "t")]
-        for sem, val, clock, src in sorted(toks, key=lambda tok: -sum(tok[2].values())):
+        toks = {tok[:2]: tok for tok in toks if not (q == "t" and tok[3] == "t") and known[q].get(tok[0], 0) < tok[1]}
+        for sem, val, clock, src in sorted(toks.values(), key=lambda tok: -sum(tok[2].values())):
             if known[q].get(sem, 0) < val:
                 queue[q].wait_ge(T.sem[sem], val)
-            for k, x in clock.items():
-                if known[q].get(k, 0) < x:
-                    known[q][k] = x
+                for k, x in clock.items():
+                    if known[q].get(k, 0) < x:
+                        known[q][k] = x
 
     def done(q, sem, n, reads, writes, src):
         total[sem] = total.get(sem, 0) + n
@@ -69,12 +78,12 @@ def make_sched(g, T):
         order(q, reads, writes)
         if more:
             call()
-            held.append((reads, writes))
+            held[q].append((reads, writes))
             return
         call().then_inc(T.sem[counter[q]], 1)
-        for rd, wr in held:
+        for rd, wr in held[q]:
             reads, writes = reads + rd, writes + wr
-        del held[:]
+        del held[q][:]
         done(q, counter[q], 1, reads, writes, q)
 
     def dma(q, out, in_, reads, writes):
@@ -100,11 +109,65 @@ def make_sched(g, T):
     return op, dma, remote, lands, finish
 
 
+def make_plan(op, dma, remote):
+    nodes, writer, readers, held, live, sent = [], {}, {}, {}, [True], []
+
+    def add(q, emit, reads, writes, busy, done, more=False):
+        if not live[0]:
+            return emit()
+        calls, rd, wr, b = held.pop(q, ([], [], [], 0.0))
+        calls, rd, wr, b = calls + [emit], rd + reads, wr + writes, b + busy
+        if more:
+            held[q] = (calls, rd, wr, b)
+            return
+        deps = {writer[k] for k in rd + wr if k in writer} | {n for k in wr for n in readers.get(k, [])}
+        for k in rd:
+            readers.setdefault(k, []).append(len(nodes))
+        for k in wr:
+            writer[k] = len(nodes); readers[k] = []
+        nodes.append((q, calls, deps, b, done))
+
+    def op2(q, call, reads, writes, more=False, busy=None):
+        add(q, lambda: op(q, call, reads, writes, more), reads, writes, busy or {"v": 0.07, "s": 0.13, "t": 0.05, "g": 0.35}[q], 0.0, more)
+
+    def dma2(q, out, in_, reads, writes, move=0.1):
+        add(q, lambda: dma(q, out, in_, reads, writes), reads, writes, 0.06, move)
+
+    def remote2(call, n, reads, arrives=(), move=0.1):
+        add("g", lambda: remote(call, n, reads), reads, list(arrives), 0.3 if sent else FIRST_CALL, move)
+        sent.append(n)
+
+    def issue():
+        live[0] = False
+        tail = [0.0] * len(nodes)
+        for n in range(len(nodes) - 1, -1, -1):
+            tail[n] += nodes[n][3] + nodes[n][4] + WAIT
+            for d in nodes[n][2]:
+                tail[d] = max(tail[d], tail[n])
+        free, end, engines, left = {}, {}, 0.0, list(range(len(nodes)))
+        while left:
+            ready = [(max([free.get(nodes[n][0], 0.0)] + [end[d] + WAIT for d in nodes[n][2]]), n) for n in left
+                     if all(d in end for d in nodes[n][2])]
+            t0, n0 = min(ready)
+            t, n = max(((t, n) for t, n in ready if nodes[n][0] == nodes[n0][0] and t <= t0 + SLACK),
+                       key=lambda x: -x[1] if nodes[n0][0] == "y" else tail[x[1]])
+            q, calls, deps, busy, move = nodes[n]
+            free[q] = end[n] = t + busy
+            if move:
+                engines = end[n] = max(engines, t + busy + 0.8) + move
+            left.remove(n)
+            for emit in calls:
+                emit()
+
+    return op2, dma2, remote2, issue
+
+
 def rank_program(g, core, T, topo):
     r = T.rank_of(core)
     if r is None:
         return
     op, dma, remote, lands, finish = make_sched(g, T)
+    op, dma, remote, issue = make_plan(op, dma, remote)
     V, S, P = g.vector, g.scalar, g.tensor
     cores = T.cores
     near = [s for s in range(N) if topo.die(cores[s]) == topo.die(core)]
@@ -112,18 +175,19 @@ def rank_program(g, core, T, topo):
     me = near.index(r)
     far_to = [far[(me + k) % len(far)] for k in range(len(far))]
     near_to = [near[(me + k) % len(near)] for k in range(1, len(near))]
-    far_from = [far[(me - k) % len(far)] for k in range(len(far))]
-    near_from = [near[(me - k) % len(near)] for k in range(1, len(near))]
     eng = topo.engines(core, cores[far[0]])
-    mask = [sum(1 << e for e in h) for h in (eng[0::2], eng[1::2])]
-    E = len(eng) // 2
+    even, odd_ = eng[0::2], eng[1::2]
+    E = len(even)
+
+    def bits(es):
+        return sum(1 << e for e in es)
 
     def dst(s):
         rid, pid, _ = topo.addr(cores[s])
         return DstId(rid=rid, pnc=pid)
 
     def to_all(src, land, sem, reads, flip):
-        ts = [RemoteDMATransfer(dst_ids=[dst(s) for s in to], dma_engine_mask=mask[k ^ flip], remote_sem=T.sem[sem],
+        ts = [RemoteDMATransfer(dst_ids=[dst(s) for s in to], dma_engine_mask=bits((even, odd_)[k ^ flip]), remote_sem=T.sem[sem],
                                 srcs=[src], dsts=[land for _ in to]) for k, to in enumerate((far_to, near_to))]
         remote(lambda: g.remote_dma_fused(ts, local_sem=T.sem.sent), 2 * E, reads)
 
@@ -133,8 +197,8 @@ def rank_program(g, core, T, topo):
         else:
             op("v", lambda: V.tensor_scalar(out, in0, s1, s2, op0, op1), reads, writes)
 
-    def tc(out, in_, reads, writes):
-        op("v", lambda: V.tensor_copy(out, in_), reads, writes)
+    def tc(out, in_, reads, writes, more=False, busy=None):
+        op("v", lambda: V.tensor_copy(out, in_), reads, writes, more, busy)
 
     def tt(out, in0, in1, o, reads, writes):
         op("v", lambda: V.tensor_tensor(out, in0, in1, o), reads, writes)
@@ -142,11 +206,11 @@ def rank_program(g, core, T, topo):
     def fill(out, x, key):
         op("v", lambda: V.memset(out, x), [], [key])
 
-    def act(out, in_, f, reads, writes, **kw):
-        op("s", lambda: S.activation(out, in_, f, **kw), reads, writes)
+    def act(out, in_, f, reads, writes, more=False, busy=None, **kw):
+        op("s", lambda: S.activation(out, in_, f, **kw), reads, writes, more, busy)
 
-    def mm(out, lhsT, rhs, start, stop, reads, writes, more=False):
-        op("t", lambda: P.matmul(out, lhsT, rhs, start, stop), reads, writes, more)
+    def mm(out, lhsT, rhs, start, stop, reads, writes, more=False, busy=None):
+        op("t", lambda: P.matmul(out, lhsT, rhs, start, stop), reads, writes, more, busy)
 
     def iota(name, pattern, cm):
         op("g", lambda: g.iota(T[name][:], pattern, 0, cm, allow_small_or_imprecise_dtypes=True), [], [name])
@@ -156,150 +220,234 @@ def rank_program(g, core, T, topo):
 
     rows = slice(16 * r, 16 * r + 16)
     part = [slice(Q * h, Q * h + Q) for h in range(SETS)]
-    order_to = [x for k in range(len(far)) for x in ([far_to[k]] + near_to[k:k + 1])]
+    others = far_to + near_to
     pair = len(eng) // N
-    lands("wd_far", "aw", (N - 1) * pair)
+    first = [sum(CHUNKS[:c]) for c in range(len(CHUNKS))]
     lands("dn_far", "an", (N - 1) * E)
     for h in range(SETS):
         lands("dv_far%d" % h, "av%d" % h, (N - 1) * E)
-    for s in order_to:
-        lands("tl%d" % s, "at%d" % s, E)
+    for c in range(len(CHUNKS)):
+        lands("X%d" % c, "ac%d" % c, 2 * E)
 
-    dma("s", T.ws[:], T.wt[:], [], ["ws"])
-    for s in order_to:
-        dma("y", T.stage[s], T.dem[16 * s:16 * s + 16, :], [], ["stage%d" % s])
+    dma("s", T.mine[:, 0:32], T.wt[:], [], ["wt"])
+    for c, nb in enumerate(CHUNKS):
+        a, b = 128 * max(first[c], 1), 128 * (first[c] + nb)
+        dma("y", T.mine[:, a:b], T.dem[:, a - 128:b - 128], [], ["mine%d" % c], 0.085 * nb)
+    rest = 8192 - 128 * PLAIN
+    dma("y", T.stage[:], T.dem[:, rest:], [], ["stage"], 0.085 * PLAIN)
+    dma("y", T.tl[r], T.dem[rows, rest:], [], ["tl_own"])
+    lands("tl", "ac7", 2 * E)
     dma("s", T.invi[0:16, :], T.inv[rows, :], [], ["invi"])
     dma("s", T.v0[:], T.v[rows, :], [], ["v0"])
     dma("s", T.supi[0:16, :], T.sup[rows, :], [], ["supi"])
-    dma("s", T.wd[r], T.wt[rows, :], [], ["wd_own"])
+    fill(T.mine[:, 32:128], 0.0, "pad")
 
+    iota("jd", [[-1, 128]], 1)
     op("g", lambda: g.iota(T.pi[:, 0:1], [[0, 1]], 0, 1), [], ["pi0"])
     iota("jm", [[0, 8], [1, 16]], 0)
-    iota("jd", [[-1, 128]], 1)
     iota("jq", [[1, 8], [8, 16]], -1)
-    wts = [RemoteDMATransfer(dst_ids=[dst(s)], dma_engine_mask=sum(1 << e for e in eng[pair * k:pair * k + pair]),
-                             remote_sem=T.sem.aw, srcs=[T.ws[s]], dsts=[T.wd[r]]) for k, s in enumerate(order_to)]
-    remote(lambda: g.remote_dma_fused(wts, local_sem=T.sem.sent), (N - 1) * pair, ["ws"])
-    for s in order_to:
-        rid, pid, _ = topo.addr(cores[s])
-        m = mask[0 if s in far else 1]
-        remote(lambda: g.remote_dma(T.tl[r], T.stage[s], T.sem["at%d" % r], T.sem.sent, pid, rid, m), E, ["stage%d" % s])
     for k in range(2):
-        op("g", lambda: g.iota(T.jp[:, 128 * k:128 * k + 128], [[1, 16], [16, 4], [128 - 256 * k, 2]], 128 * k, 0,
+        op("g", lambda k=k: g.iota(T.jp[:, 128 * k:128 * k + 128], [[1, 16], [16, 4], [128 - 256 * k, 2]], 128 * k, 0,
                                allow_small_or_imprecise_dtypes=True), [], ["jp%d" % k])
 
-    dma("s", T.wx[:], T.wd[:], ["wd_own", "wd_far"], ["wx"])
-    for k, s in enumerate(near_from):
-        dma("s", T.Y[16 * s:16 * s + 16, :], T.tl[s], ["tl%d" % s], ["Y%d" % s])
-        if k == 0:
-            dma("s", T.Y[rows, :], T.dem[rows, :], [], ["Y%d" % r])
-    for s in far_from:
-        dma("y", T.Y[16 * s:16 * s + 16, :], T.tl[s], ["tl%d" % s], ["Y%d" % s])
-    Yk = ["Y%d" % s for s in range(N)]
+    banks = {"v": ["tb0", "tb1", "tb2"], "s": ["key0", "key1"]}
 
+    def turn_blocks(c, src, reads, put, share):
+        nb = CHUNKS[c]
+        ns_ = nb * (8 - share) // 8
+        nv = min(8, (nb - ns_ + 1) // 2)
+        runs = [("s", j, min(4, ns_ - j)) for j in range(0, ns_, 4)] + [("v", j, min(nv, nb - j)) for j in range(ns_, nb, nv)]
+        for q, j0, n in runs:
+            bank = banks[q].pop(0); banks[q].append(bank)
+            for k in range(n):
+                turn_block(q, bank, T[bank][:, 128 * k:128 * k + 128], src(j0 + k), reads + ["eye"], k < n - 1)
+            put(q, j0, n, bank)
+
+    def turn_block(q, bank, out, in_, reads, more):
+        if q == "v":
+            op("t", lambda: P.transpose(out, in_, T.eye[:]), reads, [bank], more, 0.07)
+        else:
+            mm(out, in_, T.eye[:], True, True, reads, [bank], more, 0.07)
+
+    def copy(q, out, in_, reads, writes, more=False, blocks=1):
+        if q == "s":
+            act(out, in_, F.Copy, reads, writes, more, 0.13 * blocks)
+        else:
+            tc(out, in_, reads, writes, more, 0.065 * blocks)
+
+    def to_owners(c, sem, src, land, reads, arrives, move):
+        a, b = (even, odd_) if c % 2 == 0 else (odd_, even)
+        b = b if c % 4 < 2 else b[::-1]
+        es = [a[pair * k:pair * k + pair] for k in range(len(far))] + [b[0:pair], b[pair:2 * pair], b[2 * pair:]]
+        tr = [RemoteDMATransfer(dst_ids=[dst(s)], dma_engine_mask=bits(es[k]), remote_sem=T.sem[sem], srcs=[src(s)], dsts=[land])
+              for k, s in enumerate(others)]
+        remote(lambda: g.remote_dma_fused(tr, local_sem=T.sem.sent), 2 * E, reads, arrives, move)
+
+    def send(c):
+        nb, z = CHUNKS[c], 128 * first[c]
+        keys = []
+
+        def put(q, j0, n, bank):
+            keys.append("Z%d_%d" % (c, j0))
+            for k in range(n):
+                copy(q, T.Z[:, z + j0 + k:z + 128 * nb:nb], T[bank][:, 128 * k:128 * k + 128], [bank], [keys[-1] + "_%d" % k], k < n - 1)
+            keys[-1] += "_%d" % (n - 1)
+
+        turn_blocks(c, lambda j: T.mine[:, z + 128 * j:z + 128 * j + 128], ["mine%d" % c, "wt", "pad"], put, SHARE[0])
+        w = 16 * nb
+        if c == len(CHUNKS) - 1:
+            to_owners(c + 1, "ac7", lambda s: T.stage[s], T.tl[r], ["stage", "X%d" % (c - 1) + "out"], ["tl", "plain"], 0.085 * PLAIN)
+        to_owners(c, "ac%d" % c, lambda s: T.Z[:, z + w * s:z + w * s + w], T.X[:, z + w * r:z + w * r + w],
+                  keys + ["plain"], ["X%d" % c, "X%dout" % c], 0.4 + 0.085 * nb)
+        kept.append(lambda: tc(T.X[:, z + w * r:z + w * r + w], T.Z[:, z + w * r:z + w * r + w], keys, ["Xown%d" % c]))
+
+    Yk, kept = [], []
+
+    def take(c, then=None):
+        nb, z = CHUNKS[c], 128 * first[c]
+
+        def put(q, j0, n, bank):
+            Yk.append("Y%d_%d" % (c, j0))
+            copy(q, T.Y[:, z + 128 * j0:z + 128 * (j0 + n)], T[bank][:, 0:128 * n], [bank], [Yk[-1]], False, n)
+            if then and j0 == 0:
+                then()
+
+        turn_blocks(c, lambda j: T.X[:, z + j:z + 128 * nb:nb], ["X%d" % c, "Xown%d" % c], put, SHARE[1])
+
+    ts(T.eye[:], T.jd[:], 0.0, None, A.is_equal, None, ["jd"], ["eye"])
     ts(T.pi[:, 1:2], T.pi[:, 0:1], 15, None, A.bitwise_and, None, ["pi0"], ["pi1"])
     ts(T.pi[:, 2:3], T.pi[:, 0:1], 4, None, A.arith_shift_right, None, ["pi0"], ["pi2"])
     ts(T.pi[:, 3:4], T.pi[:, 0:1], Q - 1, None, A.bitwise_and, None, ["pi0"], ["pi3"])
-    tc(T.pc[:, 0:4], T.pi[:, 0:4], ["pi%d" % k for k in range(4)], ["pc"])
-    pc = [T.pc[:, k:k + 1] for k in range(16)]
-    pm, pd, pq, pb, gap, tot = pc[1:7]
-    PB, GAP, UNTIE, HALF = 4, 5, 8, 7
-    ts(pb, pm, 16.0, None, A.mult, None, ["pc"], ["pb"])
-    ts(gap, pm, -15.0, float(SPARE), A.mult, A.add, ["pc"], ["gap"])
-    ts(pc[UNTIE], pm, 16.0, -241.0, A.mult, A.add, ["pc"], ["untie"])
-    ts(T.rep[:], T.jm[:], pm, None, A.is_equal, None, ["jm", "pc"], ["rep"])
-    for name, x in (("R", 256.0), ("Rh", -65536.0), ("Rl", -256.0)):
-        ts(T[name][:], T.jm[:, 0:32], pm, x, A.is_equal, A.mult, ["jm", "pc"], [name])
-    ts(T.mk[:], T.jm[:, 0:8], pd, None, A.is_equal, None, ["jm", "pc"], ["mk"])
-    ts(T.tie[:], T.jm[:, 0:16], -16.0, 241.0, A.mult, A.add, ["jm"], ["tie"])
-    ts(T.pay[:, 0:16], T.jm[:, 0:16], -16.0, 240.0, A.mult, A.add, ["jm"], ["pay1"])
-    ts(T.cut[:], T.jm[:, 0:32], 0.0, -1.0e9, A.is_equal, A.mult, ["jm"], ["cut"])
+    ts(T.pi[:, 4:5], T.pi[:, 0:1], 4, 1, A.arith_shift_right, A.bitwise_and, ["pi0"], ["pi4"])
     fill(T.na[:, 0:1], -1.0, "na")
+    fill(T.dm[:], 0.0, "dm1")
+    fill(T.one[0:1, :], 1.0, "one")
+    for k, x in ((0, -BIG), (1, BIG)):
+        fill(T.cst[0:1, 128 * k:128 * k + 128], x, "cst%d" % k)
+    tc(T.pc[:, 0:5], T.pi[:, 0:5], ["pi%d" % k for k in range(5)], ["pc"])
     for h in range(SETS):
         for name in ("VW", "NW", "pick", "pick4"):
             fill(B(name, h)[:], 0, name + str(h))
-        ts(B("tgt", h)[:, 0:1], pm, float(SPARE), None, A.add, None, ["pc"], ["tgt%d" % h])
-    fill(T.one[0:2, :], 1.0, "one")
-    ts(pc[HALF], pc[0], -4096.5, 4096.0, A.mult, A.add, ["pc"], ["half"])
-    ts(T.cst[0:2, 0:128], T.one[0:2, :], T.pc[0:2, HALF:HALF + 1], None, A.mult, None, ["one", "half"], ["cst0"])
-    for k, x in ((1, -BIG), (2, BIG)):
-        fill(T.cst[0:1, 128 * k:128 * k + 128], x, "cst%d" % k)
+    pc = [T.pc[:, k:k + 1] for k in range(16)]
+    pm, pd, pq, odd, pb, gap, tot = pc[1:8]
+    PB, GAP, UNTIE, BYTE, HALF = 5, 6, 8, 9, 10
+    ts(pb, pm, 16.0, None, A.mult, None, ["pc"], ["pb"])
+    ts(gap, pm, -15.0, float(SPARE), A.mult, A.add, ["pc"], ["gap"])
+    ts(pc[UNTIE], pm, 16.0, -241.0, A.mult, A.add, ["pc"], ["untie"])
+    ts(pc[BYTE], odd, 65280.0, -65536.0, A.mult, A.add, ["pc"], ["byte"])
+    ts(pc[HALF + 1], pq, -4096.5, 4096.0, A.mult, A.add, ["pc"], ["half1"])
+    ts(pc[HALF + 2], pq, 2.0, None, A.is_lt, None, ["pc"], ["half2"])
+    ts(T.rep[:], T.jm[:], pm, None, A.is_equal, None, ["jm", "pc"], ["rep"])
+    ts(T.mk[:], T.jm[:, 0:8], pd, None, A.is_equal, None, ["jm", "pc"], ["mk"])
+    ts(T.unturn[:], T.jq[:], 0.0, None, A.is_equal, None, ["jq"], ["unturn"])
+    tt(pc[HALF], pc[HALF + 1], pc[HALF + 2], A.mult, ["half1", "half2"], ["half"])
+    ts(T.R[:], T.jm[:, 0:32], pm, 256.0, A.is_equal, A.mult, ["jm", "pc"], ["R"])
+    ts(T.tie[:], T.jm[:, 0:16], -16.0, 241.0, A.mult, A.add, ["jm"], ["tie"])
+    ts(T.cut[:], T.jm[:, 0:32], 0.0, -1.0e9, A.is_equal, A.mult, ["jm"], ["cut"])
     ts(T.own[:], T.mk[:], -1.0, 2.0 ** 26, A.add, A.mult, ["mk"], ["own"])
+    for h in range(SETS):
+        p, o = part[h], part[1 - h]
+        for name in ("VW", "NW"):
+            fill(B(name, h)[o, 0:1], 1.0, name + str(h))
+        ts(B("tgt", h)[:, 0:1], pm, float(SPARE), None, A.add, None, ["pc"], ["tgt%d" % h])
+        ts(B("pay", h)[p, 0:16], T.jm[p, 0:16], -16.0, 240.0, A.mult, A.add, ["jm"], ["paya%d" % h])
+        ts(B("pay", h)[o, :], T.jm[o, 0:32], T.pc[o, 1:2], T.pc[o, BYTE:BYTE + 1], A.is_equal, A.mult, ["jm", "pc", "byte"], ["payb%d" % h])
     ts(T.own[:], T.own[:], pb, None, A.add, None, ["own", "pb"], ["own"])
-    ts(T.neye[:], T.jd[:], 0.0, -1.0, A.is_equal, A.mult, ["jd"], ["neye"])
-    for name, src in (("eye", "jd"), ("unturn", "jq")):
-        ts(T[name][:], T[src][:], 0.0, None, A.is_equal, None, [src], [name])
+    send(0)
+    act(T.neye[:], T.eye[:], F.Copy, ["eye"], ["neye"], scale=-1.0)
+    for h in range(SETS):
+        for k in range(2):
+            c = 128 * (2 * h + k)
+            ts(T.sel[0:16, c:c + 128], T.jd[0:16, :], -float(Q * (1 - h) + 16 * k), None, A.is_equal, None, ["jd"], ["sel%d%d" % (h, k)])
 
     tc(T.tf[0:16, :], T.invi[0:16, :], ["invi"], ["tf"])
+    send(1)
     tc(T.invb[0:16, :], T.tf[0:16, :], ["tf"], ["invb"])
-    mm(T.m0[:, 0:16], T.invb[0:16, :], T.rep[0:16, 0:16], True, True, ["invb", "rep"], ["m0"])
-    mm(T.m1[:, 0:256], T.unturn[:], T.v0[:], True, True, ["unturn", "v0"], ["m1"])
-    tt(T.pay[:, 16:32], T.m0[:, 0:16], T.tie[:], A.add, ["m0", "tie", "pay1"], ["pay0", "pay1"])
-    op("v", lambda: V.tensor_reduce(tot, T.m0[:, 0:16], AxisListType.X, A.add), ["m0"], ["tot"])
-    ts(T.ns[:, 0:1], tot, -120.0, None, A.add, None, ["tot"], ["ns0_0", "ns1_0"])
-    for h in range(SETS):
-        ts(B("pick4", h)[part[h], :], T.own[part[h], 4 * h:4 * h + 4], T.ns[part[h], 0:1], None, A.subtract, None, ["ns0_0", "own"], ["pick4%d" % h])
-        tc(B("VW", h)[part[h], 1:257], T.m1[part[h], 0:256], ["m1"], ["VW%d" % h])
-        tc(B("wide", h)[:], B("VW", h)[:].indirect(B("pick4", h)[:]), ["VW%d" % h, "pick4%d" % h], ["wide%d" % h])
-    for name, o, x in (("suph", A.arith_shift_right, 8), ("supl", A.bitwise_and, 255)):
-        ts(T.ti[0:16, :], T.supi[0:16, :], x, None, o, None, ["supi"], ["ti"])
-        ts(T[name][0:16, :], T.ti[0:16, :], 0.0, None, A.add, None, ["ti"], [name])
-    for s in range(N):
-        ts(T.wl[:, 32 * s:32 * s + 32], T.wx[:], T.mk[:, s:s + 1], None, A.mult, None, ["wx", "mk"], ["wl%d" % s])
-    mm(T.m2[:, 0:256], T.rep[:], T.wl[:], True, True, ["rep"] + ["wl%d" % s for s in range(N)], ["m2"])
-    for eh in range(2):
-        tc(T.wr[:, 128 * eh:128 * eh + 128], T.m2[:, eh:256:2], ["m2"], ["wr%d" % eh])
-        ts(T.wn[:, 128 * eh:128 * eh + 128], T.m2[:, eh:256:2], -1.0, None, A.mult, None, ["m2"], ["wn%d" % eh])
+    ts(T.ti[0:16, :], T.supi[0:16, :], 8, None, A.arith_shift_right, None, ["supi"], ["ti"])
+    ts(T.tj[0:16, :], T.supi[0:16, :], 255, None, A.bitwise_and, None, ["supi"], ["tj"])
     ts(T.turn[:], T.jp[:], pq, None, A.is_equal, None, ["jp0", "jp1", "pc"], ["turn"])
+    ts(T.suph[0:16, :], T.ti[0:16, :], 0.0, None, A.add, None, ["ti"], ["suph"])
+    ts(T.supl[0:16, :], T.tj[0:16, :], 0.0, None, A.add, None, ["tj"], ["supl"])
+    mm(T.x1[:, 0:256], T.unturn[:], T.v0[:], True, True, ["unturn", "v0"], ["x1"])
+    mm(T.x0[:, 0:16], T.invb[0:16, :], T.rep[0:16, 0:16], True, True, ["invb", "rep"], ["x0"])
+    for h in range(SETS):
+        p, out = part[h], T.x0[:, 256 + Q * h:256 + Q * h + Q]
+        act(B("VW", h)[p, 1:257], T.x1[p, 0:256], F.Copy, ["x1"], ["VW%d" % h])
+        mm(out, T.eye[:], T.eye[:, p], True, False, ["eye"], ["x0"], True)
+        for k, name in enumerate(("suph", "supl")):
+            c = 128 * (2 * h + k)
+            mm(out, T.sel[0:16, c:c + 128], T[name][0:16, p], False, k == 1, ["sel%d%d" % (h, k), name], ["x0"], k == 0)
+    for c in range(2, len(CHUNKS)):
+        send(c)
+    op("v", lambda: V.tensor_reduce(tot, T.x0[:, 0:16], AxisListType.X, A.add), ["x0"], ["tot"])
+    kept[0]()
+    for h in range(SETS):
+        p = part[h]
+        tt(B("pay", h)[p, 16:32], T.x0[p, 0:16], T.tie[p, :], A.add, ["x0", "tie", "paya%d" % h, "payb%d" % h], ["pay%d" % h])
+        tc(B("fix", h)[:], T.x0[:, 256 + Q * h:256 + Q * h + Q], ["x0"], ["fix%d" % h])
+    ts(T.ns[:, 0:1], tot, -120.0, None, A.add, None, ["tot"], ["ns0_0", "ns1_0"])
+    for keep in kept[1:]:
+        keep()
+    for h in range(SETS):
+        o = part[1 - h]
+        ts(B("pick4", h)[part[h], :], T.own[part[h], 4 * h:4 * h + 4], T.ns[part[h], 0:1], None, A.subtract, None, ["ns0_0", "own"], ["pick4%d" % h])
+        for k in range(2):
+            act(B("wn", h)[o, 128 * k:128 * k + 128], T.jd[o, :], F.Identity, ["jd", "half"], ["wc%d%d" % (h, k)],
+                scale=0.0, bias=T.pc[o, HALF:HALF + 1])
+    for h in range(SETS):
+        tc(B("wide", h)[:], B("VW", h)[:].indirect(B("pick4", h)[:]), ["VW%d" % h, "pick4%d" % h], ["wide%d" % h])
+
+    def weights(stage):
+        if stage == 0:
+            for s in range(N):
+                ts(T.wl[:, 32 * s:32 * s + 32], T.Y[:, 0:32], T.mk[:, s:s + 1], None, A.mult, None, ["Y0_0", "mk"], ["wl%d" % s])
+            return
+        if stage == 1:
+            return mm(T.m2[:, 0:256], T.rep[:], T.wl[:], True, True, ["rep"] + ["wl%d" % s for s in range(N)], ["m2"])
+        for eh in range(2):
+            tc(T.wr[:, 128 * eh:128 * eh + 128], T.m2[:, eh:256:2], ["m2"], ["wr%d" % eh])
+            for h in range(SETS):
+                ts(B("wn", h)[part[h], 128 * eh:128 * eh + 128], T.m2[part[h], eh:256:2], -1.0, None, A.mult, None,
+                   ["m2", "wc%d%d" % (h, eh)], ["wn%d%d" % (h, eh)])
 
     def const(piece, k, more):
         a, b = PIECES[piece]
-        n = 2 if k == 0 else 1
-        mm(T["x%d" % piece][:, 0:b - a], T.one[0:n, :], T.cst[0:n, 128 * k:128 * k + b - a], k == 0, False,
+        mm(T["x%d" % piece][:, 0:b - a], T.one[0:1, :], T.cst[0:1, 128 * k:128 * k + b - a], k == 0, False,
            ["one", "cst%d" % k], ["x%d" % piece], more)
 
     def places(h, piece):
         a, b = PIECES[piece]
-        bank = "x%d" % piece
+        bank, p = "x%d" % piece, part[h]
         parts = [(c, d) for c, d in ((a, min(b, Q)), (max(a, Q), b)) if c < d]
-        for name in ("wn", "wr"):
-            for c, d in parts:
-                eh, last = c // Q, name == "wr" and d == b
-                mm(T[bank][:, c - a:d - a], T[name][:, 128 * eh:128 * eh + 128], B("wide", h)[:, c % Q:c % Q + d - c], False,
-                   last, [name + str(eh), "wide%d" % h], [bank], not last)
-            if name == "wn":
-                const(piece, 1, True)
-                const(piece, 2, True)
+        for c, d in parts:
+            mm(T[bank][:, c - a:d - a], B("wn", h)[:, 128 * (c // Q):128 * (c // Q) + 128], B("wide", h)[:, c % Q:c % Q + d - c], False,
+               False, ["wn%d%d" % (h, c // Q), "wide%d" % h], [bank], True)
+        const(piece, 1, True)
+        for c, d in parts:
+            mm(T[bank][:, c - a:d - a], T.wr[p, 128 * (c // Q):128 * (c // Q) + 128], B("wide", h)[p, c % Q:c % Q + d - c], False,
+               d == b, ["wr%d" % (c // Q)], [bank], d != b)
 
     def cols(name, h, a, b):
         return ["%s%d_%d" % (name, h, c) for c in range(a // 2, b // 2)]
 
     def look(h, q, a, b):
-        out, src = B("G", h)[:, 16 * a:16 * b], T.Y[:].indirect(B("off", h)[:, a:b])
-        reads, writes = Yk + cols("off", h, a, b), cols("G", h, a, b)
-        if q == "s":
-            act(out, src, F.Copy, reads, writes)
-        else:
-            tc(out, src, reads, writes)
+        copy(q, B("G", h)[:, 16 * a:16 * b], T.Y[:, 128:].indirect(B("off", h)[:, a:b]), Yk + cols("off", h, a, b), cols("G", h, a, b))
 
     def sums(h, a, b):
         p = Q * h + a % Q
         for e in range(16):
-            mm(B("key", h)[p:p + b - a, 0:32], B("G", h)[:, 16 * a + e:16 * b:16], T.R[:], False, False,
+            mm(B("key", h)[p:p + b - a, 0:32], B("G", h)[:, 16 * a + e:16 * b:16], T.R[:], False, a >= Q and e == 15,
                cols("G", h, a, b) + ["R"], ["key%d" % h], e < 15)
 
     def call(h, t, what):
         H, p = str(h), part[h]
-        key, VW, NW = B("key", h), B("VW", h), B("NW", h)
+        key, VW, NW, pay = B("key", h), B("VW", h), B("NW", h), B("pay", h)
         ns, np_, na, nap = T.ns[p, t + 1:t + 2], T.ns[p, t:t + 1], T.na[p, t + 1:t + 2], T.na[p, t:t + 1]
         kns, knp = "ns%d_%d" % (h, t + 1), "ns%d_%d" % (h, t)
         kna, knap = "na%d_%d" % (h, t + 1), "na%d_%d" % (h, t) if t else "na"
         m0c, mcc, base = T.sc[p, 15:16], T.sc[p, 31:32], T.pc[p, PB:PB + 1]
         if what == "fixed":
-            mm(key[p, 0:32], T.suph[0:16, p], T.Rh[0:16, :], True, False, ["suph", "Rh"], ["key" + H], True)
-            mm(key[p, 0:32], T.supl[0:16, p], T.Rl[0:16, :], False, False, ["supl", "Rl"], ["key" + H])
-        elif what == "last":
-            mm(key[p, 0:32], T.eye[p, p], T.pay[p, 0:32], False, True, ["eye", "pay" + H], ["key" + H])
+            mm(key[p, 0:32], B("fix", h)[:], pay[:], True, False, ["fix" + H, "pay" + H], ["key" + H])
         elif what == "scan":
             op("v", lambda: V.tensor_tensor_scan(T.sc[p, :], T.cut[p, :], key[p, 0:32], -1.0e9, A.add, A.max), ["cut", "key" + H], ["sc" + H])
         elif what == "pick4":
@@ -334,58 +482,74 @@ def rank_program(g, core, T, topo):
         elif what == "dl":
             ts(T.dl[p, :], key[p, 0:16], m0c, T.dd[p, 0:1], A.is_equal, A.mult, ["key" + H, "sc" + H, "dd" + H], ["dl" + H])
         elif what == "pay":
-            tt(T.pay[p, 16:32], T.pay[p, 16:32], T.dl[p, :], A.add, ["pay" + H, "dl" + H], ["pay" + H])
+            tt(pay[p, 16:32], pay[p, 16:32], T.dl[p, :], A.add, ["pay" + H, "dl" + H], ["pay" + H])
         elif what == "mirror":
-            for out, eye, src, st in ((slice(0, 256), "neye", slice(1, 257), 0), (slice(0, 256, 16), "eye", slice(16, 257, 16), 1),
+            for out, eye, src, st in ((slice(0, 256), "eye", slice(0, 256), 0), (slice(0, 256, 16), "eye", slice(16, 257, 16), 1),
                                       (slice(0, 256, 16), "neye", slice(0, 256, 16), 1), (slice(15, 256, 16), "eye", slice(1, 257, 16), 1),
-                                      (slice(15, 256, 16), "neye", slice(17, 258, 16), 1), (slice(0, 256), "eye", slice(0, 256), 1),
+                                      (slice(15, 256, 16), "neye", slice(17, 258, 16), 1), (slice(0, 256), "neye", slice(1, 257), 1),
                                       (slice(0, 256), "eye", slice(2, 258), 2)):
-                mm(T.m2[p, out], T[eye][p, p], VW[p, src], st == 0, st == 2, [eye, "VW" + H], ["m2"], st < 2)
+                mm(T.m2[p, out], T[eye][p, p], VW[p, src], st == 0, st == 2, [eye, "VW" + H], ["m2"], st != 2, 0.08)
         elif what == "NW":
-            act(NW[p, 1:257], T.m2[p, 0:256], F.Copy, ["m2"], ["NW" + H])
+            act(NW[p, 1:257], T.m2[p, 0:256], F.Copy, ["m2"], ["NW" + H], False, 0.26)
         elif what == "out":
             for k in range(2):
-                mm(T.m1[:, 0:128], T.turn[p, 128 * k:128 * k + 128], VW[p, 1 + 128 * k:129 + 128 * k], k == 0, k == 1, ["turn", "VW" + H], ["m1"], k == 0)
-            act(B("vt", h)[:], T.m1[:, 0:128], F.Copy, ["m1"], ["vt" + H])
+                mm(T.x1[:, 0:128], T.turn[p, 128 * k:128 * k + 128], VW[p, 1 + 128 * k:129 + 128 * k], k == 0, k == 1, ["turn", "VW" + H], ["x1"], k == 0)
+            act(B("vt", h)[:], T.x1[:, 0:128], F.Copy, ["x1"], ["vt" + H])
             to_all(B("vt", h)[:], B("dv", h)[r], "av" + H, ["vt" + H], 0)
         elif what == "store":
             c = slice(1024 * h, 1024 * h + 1024)
-            dma("s", T.yv[rows, c], B("vt", h)[:], ["vt" + H], ["yv_own" + H])
             if r > 0:
-                dma("y", T.yv[0:16 * r, c], B("dv", h)[0:r], ["dv_far" + H], ["yv_a" + H])
+                dma("y", T.yv[0:16 * r, c], B("dv", h)[0:r], ["dv_far" + H, "dn_own"], ["yv_a" + H])
             if r < N - 1:
-                dma("y", T.yv[16 * r + 16:128, c], B("dv", h)[r + 1:N], ["dv_far" + H], ["yv_b" + H])
+                dma("s" if r else "y", T.yv[16 * r + 16:128, c], B("dv", h)[r + 1:N], ["dv_far" + H, "dn_own"], ["yv_b" + H])
+        elif what == "own":
+            dma("y", T.yv[rows, 1024 * h:1024 * h + 1024], B("vt", h)[:], ["vt" + H], ["yv_own" + H])
+        elif what == "moved":
+            ts(T.dd[p, 0:1], ns, 0.0, np_, A.is_lt, A.mult, [kns, knp], ["dd" + H])
+        elif what == "dla":
+            ts(T.dl[p, :], key[p, 0:16], m0c, ns, A.is_equal, A.mult, ["key" + H, "sc" + H, kns], ["dl" + H])
+        elif what == "dlb":
+            ts(T.dm[p, :], key[p, 0:16], m0c, T.dd[p, 0:1], A.is_equal, A.mult, ["key" + H, "sc" + H, "dd" + H], ["dm" + H])
         elif what == "slots":
-            mm(T.m0[0:16, 0:128], T.pay[:, 16:32], T.eye[:], True, False, ["pay0", "pay1", "eye"], ["m0"], True)
-            mm(T.m0[0:16, 0:128], T.dl[:], T.eye[:], False, True, ["dl0", "dl1"], ["m0"])
-            ts(T.nt[0:16, :], T.m0[0:16, 0:128], T.pc[0:16, UNTIE:UNTIE + 1], None, A.add, None, ["m0", "untie"], ["nt"])
+            mm(T.x0[0:16, p], pay[:, 16:32], T.eye[:, p], True, False, ["pay" + H, "eye"], ["x0"])
+            mm(T.x0[0:16, p], T.dl[:], T.eye[:, p], False, False, ["dl0", "dl1"], ["x0"])
+            mm(T.x0[0:16, p], T.dm[:], T.neye[:, p], False, True, ["dm0", "dm1"], ["x0"])
+        elif what == "nt":
+            ts(T.nt[0:16, :], T.x0[0:16, 0:128], T.pc[0:16, UNTIE:UNTIE + 1], None, A.add, None, ["x0", "untie"], ["nt"])
             dma("y", T.dn[r], T.nt[0:16, :], ["nt"], ["dn_own"])
 
+    for what in ("mirror", "NW", "ahead"):
+        call(0, 0, what)
+    take(0, lambda: weights(0))
+    weights(1)
+    weights(2)
+    take(1)
     for h in range(SETS):
-        for what in ("ahead", "places", "u0", "u1", "mirror", "NW"):
+        for what in ("places", "u0", "u1", "ahead"):
             call(h, 0, what)
-    call(0, 0, "ahead")
+    for c in range(2, len(CHUNKS)):
+        take(c)
+    dma("y", T.Y[:, rest + 128:], T.tl[:], ["tl", "tl_own"], ["Yrest"], 0.085 * PLAIN)
+    Yk.append("Yrest")
+    issue()
     turns = [(h, t) for t in range(STEPS) for h in range(SETS)]
     for n, (h, t) in enumerate(turns):
-        for x in TURN if n else FIRST:
+        late = tuple(x for x in TURN if x in ("*dd", "*tgt", "*dl", "*put", "*pay"))
+        for x in FIRST if n == 0 else late + LAST if n == len(turns) - 1 else TURN:
             if x[0] == "sum":
                 sums(h, x[1], x[2])
             elif isinstance(x, tuple):
                 look(h, x[0], x[1], x[2])
             elif x[0] == "*":
-                if t or x in ("*fixed", "*last"):
-                    call(h, t - (x not in ("*fixed", "*last")), x[1:])
-            elif n < len(turns) - 1 or x not in ("pick4", "wide", "places", "u0", "u1", "mirror", "NW", "ahead", "pay"):
-                if n < len(turns) - 2 or x != "ahead":
-                    call(turns[n - 1][0], turns[n - 1][1], x)
-    for x in TURN:
-        if x in ("*na", "*dd", "*spare", "*new", "*tgt", "*dl", "*put"):
-            call(0, STEPS - 1, x[1:])
-    call(0, STEPS - 1, "out")
-    for what in ("scan", "ns", "pick", "spare", "na", "dd", "new", "tgt", "dl", "put", "slots", "out"):
+                if t or x in ("*fixed", "*mirror", "*NW"):
+                    call(h, max(0, t - (x != "*fixed")), x[1:])
+            elif n < len(turns) - 2 or x != "ahead":
+                call(turns[n - 1][0], turns[n - 1][1], x)
+    for what in END:
         call(1, STEPS - 1, what)
+    call(0, STEPS - 1, "store")
     to_all(T.dn[r], T.dn[r], "an", ["dn_own"], 1)
-    for h in range(SETS):
-        call(h, STEPS - 1, "store")
-    dma("s", T.yi[:], T.dn[:], ["dn_own", "dn_far"], ["yi"])
+    call(1, STEPS - 1, "own")
+    call(1, STEPS - 1, "store")
+    dma("y", T.yi[:], T.dn[:], ["dn_own", "dn_far"], ["yi"])
     finish()

from concourse.bass import DstId, RemoteDMATransfer
from concourse.mybir import AluOpType as A, AxisListType, ActivationFunctionType as F

N, STEPS, SETS, Q = 8, 5, 2, 64
VWID, SPARE = 288, 258
BIG = 1.5 * 2.0 ** 36
PLAIN = 20
CHUNKS = (13, 20, 12)
SHARE = (4, 6)
WAIT, SLACK, FIRST_CALL = 0.22, 0.1, 1.8
PIECES = ((0, 64), (64, 128))
TURN = (("s", 0, 36), "*fixed", "*mirror", ("v", 36, 58), "scan", ("v", 58, 64), ("s", 64, 94), "pick4", "ns", "pick", "wide",
        ("sum", 0, 64), "spare", "places", "na", ("s", 94, 104), ("v", 104, 128), "dd", "new", ("sum", 64, 96), "*NW", "tgt",
        "u0", "dl", ("sum", 96, 128), "u1", "put", "ahead", "pay")
LAST = (("v", 32, 56), ("s", 0, 32), ("s", 64, 96), "scan", ("v", 56, 64), "ns", "pick", "*fixed", "*mirror",
        ("sum", 0, 64), ("v", 102, 116), "spare", "new", "moved", ("s", 96, 102), ("v", 116, 128), "tgt", "dla", "dlb", ("sum", 64, 96),
        "put", ("sum", 96, 128), "*NW", "out", "own", "slots")
END = ("scan", "ns", "pick", "spare", "new", "moved", "dla", "tgt", "dlb", "put", "slots", "out", "nt")
FIRST = (("s", 0, 32), ("v", 32, 64), ("s", 64, 96), ("v", 96, 128), "*fixed", ("sum", 0, 64), ("sum", 64, 128))
BF, FP, I32, U16 = "bfloat16", "float32", "int32", "uint16"
SCRATCH = {"dn": ("dram", [N, 128, 16], FP), "stage": ("dram", [N, 128, 16 * PLAIN], BF), "tl": ("dram", [N, 128, 16 * PLAIN], BF)}
for _dt, _bufs in ((BF, dict(mine=8320, Z=8320, X=8320, Y=8320, wl=256, wr=256, v0=256, invb=128, suph=128, supl=128,
                             eye=128, neye=128, unturn=128, turn=256, rep=128, R=32, sel=512, dl=16, dm=16, one=128, cst=256,
                             jm=128, jd=128, jp=256, jq=128)),
                   (FP, dict(tf=128, pc=16, mk=8, cut=32, tie=16, sc=32, sv=8,
                             ns=8, na=8, dd=8, nt=128, own=8)),
                   (I32, dict(invi=128, supi=128, ti=128, tj=128, pi=8))):
    for _name, _cols in _bufs.items():
        SCRATCH[_name] = ("sbuf", [128, _cols], _dt)
for _h in range(SETS):
    SCRATCH["dv%d" % _h] = ("dram", [N, 128, 128], BF)
    for _dt, _bufs in ((BF, dict(G=32 * Q, VW=VWID, NW=VWID, wide=Q, new=16, vt=128, wn=256, fix=Q, pay=32)),
                       (U16, dict(off=2 * Q, pick=2, tgt=2, pick4=4))):
        for _name, _cols in _bufs.items():
            SCRATCH[_name + str(_h)] = ("sbuf", [128, _cols], _dt)
PSUM = ("x0", "x1", "key0", "key1", "m2", "tb0", "tb1", "tb2")
for _name in PSUM:
    SCRATCH[_name] = ("psum", [128, 1024], BF) if _name[0] == "t" else ("psum", [128, 512], FP)
SEMAPHORES = (["cg", "cv", "cs", "ct", "sent", "av0", "av1", "an"] + ["ac%d" % c for c in range(8)]
              + ["d%d" % k for k in range(32)])


def make_sched(g, T):
    queue = {"g": g, "v": g.vector, "s": g.scalar, "t": g.tensor, "y": g.sync}
    counter = {"g": "cg", "v": "cv", "s": "cs", "t": "ct"}
    total, known, writer, readers, ndma = {}, {q: {} for q in queue}, {}, {}, [0]
    held = {q: [] for q in queue}

    def order(q, reads, writes):
        toks = []
        for k in reads:
            if k in writer:
                toks.append(writer[k])
            if k in PSUM:
                toks += [tok for tok in readers.get(k, []) if tok[3] != q]
        for k in writes:
            if k in writer:
                toks.append(writer[k])
            toks += readers.get(k, [])
        toks = {tok[:2]: tok for tok in toks if not (q == "t" and tok[3] == "t") and known[q].get(tok[0], 0) < tok[1]}
        for sem, val, clock, src in sorted(toks.values(), key=lambda tok: -sum(tok[2].values())):
            if known[q].get(sem, 0) < val:
                queue[q].wait_ge(T.sem[sem], val)
                for k, x in clock.items():
                    if known[q].get(k, 0) < x:
                        known[q][k] = x

    def done(q, sem, n, reads, writes, src):
        total[sem] = total.get(sem, 0) + n
        clock = dict(known[q]); clock[sem] = total[sem]
        tok = (sem, total[sem], clock, src)
        for k in reads:
            readers.setdefault(k, []).append(tok)
        for k in writes:
            writer[k] = tok; readers[k] = []

    def op(q, call, reads, writes, more=False):
        order(q, reads, writes)
        if more:
            call()
            held[q].append((reads, writes))
            return
        call().then_inc(T.sem[counter[q]], 1)
        for rd, wr in held[q]:
            reads, writes = reads + rd, writes + wr
        del held[q][:]
        done(q, counter[q], 1, reads, writes, q)

    def dma(q, out, in_, reads, writes):
        order(q, reads, writes)
        sem = "d%d" % ndma[0]; ndma[0] += 1
        queue[q].dma_start(out, in_).then_inc(T.sem[sem], 16)
        done(q, sem, 16, reads, writes, "dma")

    def remote(call, n, reads):
        order("g", reads, [])
        call()
        total["sent"] = total.get("sent", 0) + n

    def lands(key, sem, n):
        total[sem] = n
        writer[key] = (sem, n, {sem: n}, "far")

    def finish():
        for sem, n in total.items():
            if known["g"].get(sem, 0) < n:
                g.wait_ge(T.sem[sem], n)

    return op, dma, remote, lands, finish


def make_plan(op, dma, remote):
    nodes, writer, readers, held, live, sent = [], {}, {}, {}, [True], []

    def add(q, emit, reads, writes, busy, done, more=False):
        if not live[0]:
            return emit()
        calls, rd, wr, b = held.pop(q, ([], [], [], 0.0))
        calls, rd, wr, b = calls + [emit], rd + reads, wr + writes, b + busy
        if more:
            held[q] = (calls, rd, wr, b)
            return
        deps = {writer[k] for k in rd + wr if k in writer} | {n for k in wr for n in readers.get(k, [])}
        for k in rd:
            readers.setdefault(k, []).append(len(nodes))
        for k in wr:
            writer[k] = len(nodes); readers[k] = []
        nodes.append((q, calls, deps, b, done))

    def op2(q, call, reads, writes, more=False, busy=None):
        add(q, lambda: op(q, call, reads, writes, more), reads, writes, busy or {"v": 0.07, "s": 0.13, "t": 0.05, "g": 0.35}[q], 0.0, more)

    def dma2(q, out, in_, reads, writes, move=0.1):
        add(q, lambda: dma(q, out, in_, reads, writes), reads, writes, 0.06, move)

    def remote2(call, n, reads, arrives=(), move=0.1):
        add("g", lambda: remote(call, n, reads), reads, list(arrives), 0.3 if sent else FIRST_CALL, move)
        sent.append(n)

    def issue():
        live[0] = False
        tail = [0.0] * len(nodes)
        for n in range(len(nodes) - 1, -1, -1):
            tail[n] += nodes[n][3] + nodes[n][4] + WAIT
            for d in nodes[n][2]:
                tail[d] = max(tail[d], tail[n])
        free, end, engines, left = {}, {}, 0.0, list(range(len(nodes)))
        while left:
            ready = [(max([free.get(nodes[n][0], 0.0)] + [end[d] + WAIT for d in nodes[n][2]]), n) for n in left
                     if all(d in end for d in nodes[n][2])]
            t0, n0 = min(ready)
            t, n = max(((t, n) for t, n in ready if nodes[n][0] == nodes[n0][0] and t <= t0 + SLACK),
                       key=lambda x: -x[1] if nodes[n0][0] == "y" else tail[x[1]])
            q, calls, deps, busy, move = nodes[n]
            free[q] = end[n] = t + busy
            if move:
                engines = end[n] = max(engines, t + busy + 0.8) + move
            left.remove(n)
            for emit in calls:
                emit()

    return op2, dma2, remote2, issue


def rank_program(g, core, T, topo):
    r = T.rank_of(core)
    if r is None:
        return
    op, dma, remote, lands, finish = make_sched(g, T)
    op, dma, remote, issue = make_plan(op, dma, remote)
    V, S, P = g.vector, g.scalar, g.tensor
    cores = T.cores
    near = [s for s in range(N) if topo.die(cores[s]) == topo.die(core)]
    far = [s for s in range(N) if topo.die(cores[s]) != topo.die(core)]
    me = near.index(r)
    far_to = [far[(me + k) % len(far)] for k in range(len(far))]
    near_to = [near[(me + k) % len(near)] for k in range(1, len(near))]
    eng = topo.engines(core, cores[far[0]])
    even, odd_ = eng[0::2], eng[1::2]
    E = len(even)

    def bits(es):
        return sum(1 << e for e in es)

    def dst(s):
        rid, pid, _ = topo.addr(cores[s])
        return DstId(rid=rid, pnc=pid)

    def to_all(src, land, sem, reads, flip):
        ts = [RemoteDMATransfer(dst_ids=[dst(s) for s in to], dma_engine_mask=bits((even, odd_)[k ^ flip]), remote_sem=T.sem[sem],
                                srcs=[src], dsts=[land for _ in to]) for k, to in enumerate((far_to, near_to))]
        remote(lambda: g.remote_dma_fused(ts, local_sem=T.sem.sent), 2 * E, reads)

    def ts(out, in0, s1, s2, op0, op1, reads, writes):
        if op1 is None:
            op("v", lambda: V.tensor_scalar(out, in0, s1, None, op0), reads, writes)
        else:
            op("v", lambda: V.tensor_scalar(out, in0, s1, s2, op0, op1), reads, writes)

    def tc(out, in_, reads, writes, more=False, busy=None):
        op("v", lambda: V.tensor_copy(out, in_), reads, writes, more, busy)

    def tt(out, in0, in1, o, reads, writes):
        op("v", lambda: V.tensor_tensor(out, in0, in1, o), reads, writes)

    def fill(out, x, key):
        op("v", lambda: V.memset(out, x), [], [key])

    def act(out, in_, f, reads, writes, more=False, busy=None, **kw):
        op("s", lambda: S.activation(out, in_, f, **kw), reads, writes, more, busy)

    def mm(out, lhsT, rhs, start, stop, reads, writes, more=False, busy=None):
        op("t", lambda: P.matmul(out, lhsT, rhs, start, stop), reads, writes, more, busy)

    def iota(name, pattern, cm):
        op("g", lambda: g.iota(T[name][:], pattern, 0, cm, allow_small_or_imprecise_dtypes=True), [], [name])

    def B(name, h):
        return T[name + str(h)]

    rows = slice(16 * r, 16 * r + 16)
    part = [slice(Q * h, Q * h + Q) for h in range(SETS)]
    others = far_to + near_to
    pair = len(eng) // N
    first = [sum(CHUNKS[:c]) for c in range(len(CHUNKS))]
    lands("dn_far", "an", (N - 1) * E)
    for h in range(SETS):
        lands("dv_far%d" % h, "av%d" % h, (N - 1) * E)
    for c in range(len(CHUNKS)):
        lands("X%d" % c, "ac%d" % c, 2 * E)

    dma("s", T.mine[:, 0:32], T.wt[:], [], ["wt"])
    for c, nb in enumerate(CHUNKS):
        a, b = 128 * max(first[c], 1), 128 * (first[c] + nb)
        dma("y", T.mine[:, a:b], T.dem[:, a - 128:b - 128], [], ["mine%d" % c], 0.085 * nb)
    rest = 8192 - 128 * PLAIN
    dma("y", T.stage[:], T.dem[:, rest:], [], ["stage"], 0.085 * PLAIN)
    dma("y", T.tl[r], T.dem[rows, rest:], [], ["tl_own"])
    lands("tl", "ac7", 2 * E)
    dma("s", T.invi[0:16, :], T.inv[rows, :], [], ["invi"])
    dma("s", T.v0[:], T.v[rows, :], [], ["v0"])
    dma("s", T.supi[0:16, :], T.sup[rows, :], [], ["supi"])
    fill(T.mine[:, 32:128], 0.0, "pad")

    iota("jd", [[-1, 128]], 1)
    op("g", lambda: g.iota(T.pi[:, 0:1], [[0, 1]], 0, 1), [], ["pi0"])
    iota("jm", [[0, 8], [1, 16]], 0)
    iota("jq", [[1, 8], [8, 16]], -1)
    for k in range(2):
        op("g", lambda k=k: g.iota(T.jp[:, 128 * k:128 * k + 128], [[1, 16], [16, 4], [128 - 256 * k, 2]], 128 * k, 0,
                               allow_small_or_imprecise_dtypes=True), [], ["jp%d" % k])

    banks = {"v": ["tb0", "tb1", "tb2"], "s": ["key0", "key1"]}

    def turn_blocks(c, src, reads, put, share):
        nb = CHUNKS[c]
        ns_ = nb * (8 - share) // 8
        nv = min(8, (nb - ns_ + 1) // 2)
        runs = [("s", j, min(4, ns_ - j)) for j in range(0, ns_, 4)] + [("v", j, min(nv, nb - j)) for j in range(ns_, nb, nv)]
        for q, j0, n in runs:
            bank = banks[q].pop(0); banks[q].append(bank)
            for k in range(n):
                turn_block(q, bank, T[bank][:, 128 * k:128 * k + 128], src(j0 + k), reads + ["eye"], k < n - 1)
            put(q, j0, n, bank)

    def turn_block(q, bank, out, in_, reads, more):
        if q == "v":
            op("t", lambda: P.transpose(out, in_, T.eye[:]), reads, [bank], more, 0.07)
        else:
            mm(out, in_, T.eye[:], True, True, reads, [bank], more, 0.07)

    def copy(q, out, in_, reads, writes, more=False, blocks=1):
        if q == "s":
            act(out, in_, F.Copy, reads, writes, more, 0.13 * blocks)
        else:
            tc(out, in_, reads, writes, more, 0.065 * blocks)

    def to_owners(c, sem, src, land, reads, arrives, move):
        a, b = (even, odd_) if c % 2 == 0 else (odd_, even)
        b = b if c % 4 < 2 else b[::-1]
        es = [a[pair * k:pair * k + pair] for k in range(len(far))] + [b[0:pair], b[pair:2 * pair], b[2 * pair:]]
        tr = [RemoteDMATransfer(dst_ids=[dst(s)], dma_engine_mask=bits(es[k]), remote_sem=T.sem[sem], srcs=[src(s)], dsts=[land])
              for k, s in enumerate(others)]
        remote(lambda: g.remote_dma_fused(tr, local_sem=T.sem.sent), 2 * E, reads, arrives, move)

    def send(c):
        nb, z = CHUNKS[c], 128 * first[c]
        keys = []

        def put(q, j0, n, bank):
            keys.append("Z%d_%d" % (c, j0))
            for k in range(n):
                copy(q, T.Z[:, z + j0 + k:z + 128 * nb:nb], T[bank][:, 128 * k:128 * k + 128], [bank], [keys[-1] + "_%d" % k], k < n - 1)
            keys[-1] += "_%d" % (n - 1)

        turn_blocks(c, lambda j: T.mine[:, z + 128 * j:z + 128 * j + 128], ["mine%d" % c, "wt", "pad"], put, SHARE[0])
        w = 16 * nb
        if c == len(CHUNKS) - 1:
            to_owners(c + 1, "ac7", lambda s: T.stage[s], T.tl[r], ["stage", "X%d" % (c - 1) + "out"], ["tl", "plain"], 0.085 * PLAIN)
        to_owners(c, "ac%d" % c, lambda s: T.Z[:, z + w * s:z + w * s + w], T.X[:, z + w * r:z + w * r + w],
                  keys + ["plain"], ["X%d" % c, "X%dout" % c], 0.4 + 0.085 * nb)
        kept.append(lambda: tc(T.X[:, z + w * r:z + w * r + w], T.Z[:, z + w * r:z + w * r + w], keys, ["Xown%d" % c]))

    Yk, kept = [], []

    def take(c, then=None):
        nb, z = CHUNKS[c], 128 * first[c]

        def put(q, j0, n, bank):
            Yk.append("Y%d_%d" % (c, j0))
            copy(q, T.Y[:, z + 128 * j0:z + 128 * (j0 + n)], T[bank][:, 0:128 * n], [bank], [Yk[-1]], False, n)
            if then and j0 == 0:
                then()

        turn_blocks(c, lambda j: T.X[:, z + j:z + 128 * nb:nb], ["X%d" % c, "Xown%d" % c], put, SHARE[1])

    ts(T.eye[:], T.jd[:], 0.0, None, A.is_equal, None, ["jd"], ["eye"])
    ts(T.pi[:, 1:2], T.pi[:, 0:1], 15, None, A.bitwise_and, None, ["pi0"], ["pi1"])
    ts(T.pi[:, 2:3], T.pi[:, 0:1], 4, None, A.arith_shift_right, None, ["pi0"], ["pi2"])
    ts(T.pi[:, 3:4], T.pi[:, 0:1], Q - 1, None, A.bitwise_and, None, ["pi0"], ["pi3"])
    ts(T.pi[:, 4:5], T.pi[:, 0:1], 4, 1, A.arith_shift_right, A.bitwise_and, ["pi0"], ["pi4"])
    fill(T.na[:, 0:1], -1.0, "na")
    fill(T.dm[:], 0.0, "dm1")
    fill(T.one[0:1, :], 1.0, "one")
    for k, x in ((0, -BIG), (1, BIG)):
        fill(T.cst[0:1, 128 * k:128 * k + 128], x, "cst%d" % k)
    tc(T.pc[:, 0:5], T.pi[:, 0:5], ["pi%d" % k for k in range(5)], ["pc"])
    for h in range(SETS):
        for name in ("VW", "NW", "pick", "pick4"):
            fill(B(name, h)[:], 0, name + str(h))
    pc = [T.pc[:, k:k + 1] for k in range(16)]
    pm, pd, pq, odd, pb, gap, tot = pc[1:8]
    PB, GAP, UNTIE, BYTE, HALF = 5, 6, 8, 9, 10
    ts(pb, pm, 16.0, None, A.mult, None, ["pc"], ["pb"])
    ts(gap, pm, -15.0, float(SPARE), A.mult, A.add, ["pc"], ["gap"])
    ts(pc[UNTIE], pm, 16.0, -241.0, A.mult, A.add, ["pc"], ["untie"])
    ts(pc[BYTE], odd, 65280.0, -65536.0, A.mult, A.add, ["pc"], ["byte"])
    ts(pc[HALF + 1], pq, -4096.5, 4096.0, A.mult, A.add, ["pc"], ["half1"])
    ts(pc[HALF + 2], pq, 2.0, None, A.is_lt, None, ["pc"], ["half2"])
    ts(T.rep[:], T.jm[:], pm, None, A.is_equal, None, ["jm", "pc"], ["rep"])
    ts(T.mk[:], T.jm[:, 0:8], pd, None, A.is_equal, None, ["jm", "pc"], ["mk"])
    ts(T.unturn[:], T.jq[:], 0.0, None, A.is_equal, None, ["jq"], ["unturn"])
    tt(pc[HALF], pc[HALF + 1], pc[HALF + 2], A.mult, ["half1", "half2"], ["half"])
    ts(T.R[:], T.jm[:, 0:32], pm, 256.0, A.is_equal, A.mult, ["jm", "pc"], ["R"])
    ts(T.tie[:], T.jm[:, 0:16], -16.0, 241.0, A.mult, A.add, ["jm"], ["tie"])
    ts(T.cut[:], T.jm[:, 0:32], 0.0, -1.0e9, A.is_equal, A.mult, ["jm"], ["cut"])
    ts(T.own[:], T.mk[:], -1.0, 2.0 ** 26, A.add, A.mult, ["mk"], ["own"])
    for h in range(SETS):
        p, o = part[h], part[1 - h]
        for name in ("VW", "NW"):
            fill(B(name, h)[o, 0:1], 1.0, name + str(h))
        ts(B("tgt", h)[:, 0:1], pm, float(SPARE), None, A.add, None, ["pc"], ["tgt%d" % h])
        ts(B("pay", h)[p, 0:16], T.jm[p, 0:16], -16.0, 240.0, A.mult, A.add, ["jm"], ["paya%d" % h])
        ts(B("pay", h)[o, :], T.jm[o, 0:32], T.pc[o, 1:2], T.pc[o, BYTE:BYTE + 1], A.is_equal, A.mult, ["jm", "pc", "byte"], ["payb%d" % h])
    ts(T.own[:], T.own[:], pb, None, A.add, None, ["own", "pb"], ["own"])
    send(0)
    act(T.neye[:], T.eye[:], F.Copy, ["eye"], ["neye"], scale=-1.0)
    for h in range(SETS):
        for k in range(2):
            c = 128 * (2 * h + k)
            ts(T.sel[0:16, c:c + 128], T.jd[0:16, :], -float(Q * (1 - h) + 16 * k), None, A.is_equal, None, ["jd"], ["sel%d%d" % (h, k)])

    tc(T.tf[0:16, :], T.invi[0:16, :], ["invi"], ["tf"])
    send(1)
    tc(T.invb[0:16, :], T.tf[0:16, :], ["tf"], ["invb"])
    ts(T.ti[0:16, :], T.supi[0:16, :], 8, None, A.arith_shift_right, None, ["supi"], ["ti"])
    ts(T.tj[0:16, :], T.supi[0:16, :], 255, None, A.bitwise_and, None, ["supi"], ["tj"])
    ts(T.turn[:], T.jp[:], pq, None, A.is_equal, None, ["jp0", "jp1", "pc"], ["turn"])
    ts(T.suph[0:16, :], T.ti[0:16, :], 0.0, None, A.add, None, ["ti"], ["suph"])
    ts(T.supl[0:16, :], T.tj[0:16, :], 0.0, None, A.add, None, ["tj"], ["supl"])
    mm(T.x1[:, 0:256], T.unturn[:], T.v0[:], True, True, ["unturn", "v0"], ["x1"])
    mm(T.x0[:, 0:16], T.invb[0:16, :], T.rep[0:16, 0:16], True, True, ["invb", "rep"], ["x0"])
    for h in range(SETS):
        p, out = part[h], T.x0[:, 256 + Q * h:256 + Q * h + Q]
        act(B("VW", h)[p, 1:257], T.x1[p, 0:256], F.Copy, ["x1"], ["VW%d" % h])
        mm(out, T.eye[:], T.eye[:, p], True, False, ["eye"], ["x0"], True)
        for k, name in enumerate(("suph", "supl")):
            c = 128 * (2 * h + k)
            mm(out, T.sel[0:16, c:c + 128], T[name][0:16, p], False, k == 1, ["sel%d%d" % (h, k), name], ["x0"], k == 0)
    for c in range(2, len(CHUNKS)):
        send(c)
    op("v", lambda: V.tensor_reduce(tot, T.x0[:, 0:16], AxisListType.X, A.add), ["x0"], ["tot"])
    kept[0]()
    for h in range(SETS):
        p = part[h]
        tt(B("pay", h)[p, 16:32], T.x0[p, 0:16], T.tie[p, :], A.add, ["x0", "tie", "paya%d" % h, "payb%d" % h], ["pay%d" % h])
        tc(B("fix", h)[:], T.x0[:, 256 + Q * h:256 + Q * h + Q], ["x0"], ["fix%d" % h])
    ts(T.ns[:, 0:1], tot, -120.0, None, A.add, None, ["tot"], ["ns0_0", "ns1_0"])
    for keep in kept[1:]:
        keep()
    for h in range(SETS):
        o = part[1 - h]
        ts(B("pick4", h)[part[h], :], T.own[part[h], 4 * h:4 * h + 4], T.ns[part[h], 0:1], None, A.subtract, None, ["ns0_0", "own"], ["pick4%d" % h])
        for k in range(2):
            act(B("wn", h)[o, 128 * k:128 * k + 128], T.jd[o, :], F.Identity, ["jd", "half"], ["wc%d%d" % (h, k)],
                scale=0.0, bias=T.pc[o, HALF:HALF + 1])
    for h in range(SETS):
        tc(B("wide", h)[:], B("VW", h)[:].indirect(B("pick4", h)[:]), ["VW%d" % h, "pick4%d" % h], ["wide%d" % h])

    def weights(stage):
        if stage == 0:
            for s in range(N):
                ts(T.wl[:, 32 * s:32 * s + 32], T.Y[:, 0:32], T.mk[:, s:s + 1], None, A.mult, None, ["Y0_0", "mk"], ["wl%d" % s])
            return
        if stage == 1:
            return mm(T.m2[:, 0:256], T.rep[:], T.wl[:], True, True, ["rep"] + ["wl%d" % s for s in range(N)], ["m2"])
        for eh in range(2):
            tc(T.wr[:, 128 * eh:128 * eh + 128], T.m2[:, eh:256:2], ["m2"], ["wr%d" % eh])
            for h in range(SETS):
                ts(B("wn", h)[part[h], 128 * eh:128 * eh + 128], T.m2[part[h], eh:256:2], -1.0, None, A.mult, None,
                   ["m2", "wc%d%d" % (h, eh)], ["wn%d%d" % (h, eh)])

    def const(piece, k, more):
        a, b = PIECES[piece]
        mm(T["x%d" % piece][:, 0:b - a], T.one[0:1, :], T.cst[0:1, 128 * k:128 * k + b - a], k == 0, False,
           ["one", "cst%d" % k], ["x%d" % piece], more)

    def places(h, piece):
        a, b = PIECES[piece]
        bank, p = "x%d" % piece, part[h]
        parts = [(c, d) for c, d in ((a, min(b, Q)), (max(a, Q), b)) if c < d]
        for c, d in parts:
            mm(T[bank][:, c - a:d - a], B("wn", h)[:, 128 * (c // Q):128 * (c // Q) + 128], B("wide", h)[:, c % Q:c % Q + d - c], False,
               False, ["wn%d%d" % (h, c // Q), "wide%d" % h], [bank], True)
        const(piece, 1, True)
        for c, d in parts:
            mm(T[bank][:, c - a:d - a], T.wr[p, 128 * (c // Q):128 * (c // Q) + 128], B("wide", h)[p, c % Q:c % Q + d - c], False,
               d == b, ["wr%d" % (c // Q)], [bank], d != b)

    def cols(name, h, a, b):
        return ["%s%d_%d" % (name, h, c) for c in range(a // 2, b // 2)]

    def look(h, q, a, b):
        copy(q, B("G", h)[:, 16 * a:16 * b], T.Y[:, 128:].indirect(B("off", h)[:, a:b]), Yk + cols("off", h, a, b), cols("G", h, a, b))

    def sums(h, a, b):
        p = Q * h + a % Q
        for e in range(16):
            mm(B("key", h)[p:p + b - a, 0:32], B("G", h)[:, 16 * a + e:16 * b:16], T.R[:], False, a >= Q and e == 15,
               cols("G", h, a, b) + ["R"], ["key%d" % h], e < 15)

    def call(h, t, what):
        H, p = str(h), part[h]
        key, VW, NW, pay = B("key", h), B("VW", h), B("NW", h), B("pay", h)
        ns, np_, na, nap = T.ns[p, t + 1:t + 2], T.ns[p, t:t + 1], T.na[p, t + 1:t + 2], T.na[p, t:t + 1]
        kns, knp = "ns%d_%d" % (h, t + 1), "ns%d_%d" % (h, t)
        kna, knap = "na%d_%d" % (h, t + 1), "na%d_%d" % (h, t) if t else "na"
        m0c, mcc, base = T.sc[p, 15:16], T.sc[p, 31:32], T.pc[p, PB:PB + 1]
        if what == "fixed":
            mm(key[p, 0:32], B("fix", h)[:], pay[:], True, False, ["fix" + H, "pay" + H], ["key" + H])
        elif what == "scan":
            op("v", lambda: V.tensor_tensor_scan(T.sc[p, :], T.cut[p, :], key[p, 0:32], -1.0e9, A.add, A.max), ["cut", "key" + H], ["sc" + H])
        elif what == "pick4":
            ts(B("pick4", h)[p, :], T.own[p, 4 * h:4 * h + 4], mcc, m0c, A.add, A.subtract, ["sc" + H, "own"], ["pick4" + H])
        elif what == "wide":
            tc(B("wide", h)[:], NW[:].indirect(B("pick4", h)[:]), ["NW" + H, "pick4" + H], ["wide" + H])
        elif what == "ahead":
            for piece in range(len(PIECES)):
                const(piece, 0, False)
        elif what == "places":
            for piece in range(len(PIECES)):
                places(h, piece)
        elif what in ("u0", "u1"):
            a, b = PIECES[int(what[1])]
            tc(B("off", h)[:, a:b], T["x" + what[1]][:, 0:b - a], ["x" + what[1]], cols("off", h, a, b))
        elif what == "ns":
            ts(ns, mcc, m0c, nap, A.subtract, A.mult, ["sc" + H, knap], [kns])
        elif what == "na":
            act(na, ns, F.Sign, [kns], [kna])
        elif what == "dd":
            act(T.dd[p, 0:1], np_, F.Identity, [knp, kna, kns], ["dd" + H], bias=ns, scale=na)
        elif what == "pick":
            ts(B("pick", h)[p, 0:1], mcc, m0c, base, A.subtract, A.add, ["sc" + H, "pb"], ["pick" + H])
        elif what == "new":
            tc(B("new", h)[:], NW[:].indirect(B("pick", h)[:, 0:1]), ["NW" + H, "pick" + H], ["new" + H])
        elif what == "spare":
            ts(T.sv[p, 0:1], ns, 0.0, T.pc[p, GAP:GAP + 1], A.is_equal, A.mult, [kns, "gap"], ["sv" + H])
        elif what == "tgt":
            ts(B("tgt", h)[p, 0:1], T.sv[p, 0:1], ns, base, A.subtract, A.add, [kns, "sv" + H, "pb"], ["tgt" + H])
        elif what == "put":
            tc(VW[:].indirect(B("tgt", h)[:, 0:1]), B("new", h)[:], ["tgt" + H, "new" + H], ["VW" + H])
        elif what == "dl":
            ts(T.dl[p, :], key[p, 0:16], m0c, T.dd[p, 0:1], A.is_equal, A.mult, ["key" + H, "sc" + H, "dd" + H], ["dl" + H])
        elif what == "pay":
            tt(pay[p, 16:32], pay[p, 16:32], T.dl[p, :], A.add, ["pay" + H, "dl" + H], ["pay" + H])
        elif what == "mirror":
            for out, eye, src, st in ((slice(0, 256), "eye", slice(0, 256), 0), (slice(0, 256, 16), "eye", slice(16, 257, 16), 1),
                                      (slice(0, 256, 16), "neye", slice(0, 256, 16), 1), (slice(15, 256, 16), "eye", slice(1, 257, 16), 1),
                                      (slice(15, 256, 16), "neye", slice(17, 258, 16), 1), (slice(0, 256), "neye", slice(1, 257), 1),
                                      (slice(0, 256), "eye", slice(2, 258), 2)):
                mm(T.m2[p, out], T[eye][p, p], VW[p, src], st == 0, st == 2, [eye, "VW" + H], ["m2"], st != 2, 0.08)
        elif what == "NW":
            act(NW[p, 1:257], T.m2[p, 0:256], F.Copy, ["m2"], ["NW" + H], False, 0.26)
        elif what == "out":
            for k in range(2):
                mm(T.x1[:, 0:128], T.turn[p, 128 * k:128 * k + 128], VW[p, 1 + 128 * k:129 + 128 * k], k == 0, k == 1, ["turn", "VW" + H], ["x1"], k == 0)
            act(B("vt", h)[:], T.x1[:, 0:128], F.Copy, ["x1"], ["vt" + H])
            to_all(B("vt", h)[:], B("dv", h)[r], "av" + H, ["vt" + H], 0)
        elif what == "store":
            c = slice(1024 * h, 1024 * h + 1024)
            if r > 0:
                dma("y", T.yv[0:16 * r, c], B("dv", h)[0:r], ["dv_far" + H, "dn_own"], ["yv_a" + H])
            if r < N - 1:
                dma("s" if r else "y", T.yv[16 * r + 16:128, c], B("dv", h)[r + 1:N], ["dv_far" + H, "dn_own"], ["yv_b" + H])
        elif what == "own":
            dma("y", T.yv[rows, 1024 * h:1024 * h + 1024], B("vt", h)[:], ["vt" + H], ["yv_own" + H])
        elif what == "moved":
            ts(T.dd[p, 0:1], ns, 0.0, np_, A.is_lt, A.mult, [kns, knp], ["dd" + H])
        elif what == "dla":
            ts(T.dl[p, :], key[p, 0:16], m0c, ns, A.is_equal, A.mult, ["key" + H, "sc" + H, kns], ["dl" + H])
        elif what == "dlb":
            ts(T.dm[p, :], key[p, 0:16], m0c, T.dd[p, 0:1], A.is_equal, A.mult, ["key" + H, "sc" + H, "dd" + H], ["dm" + H])
        elif what == "slots":
            mm(T.x0[0:16, p], pay[:, 16:32], T.eye[:, p], True, False, ["pay" + H, "eye"], ["x0"])
            mm(T.x0[0:16, p], T.dl[:], T.eye[:, p], False, False, ["dl0", "dl1"], ["x0"])
            mm(T.x0[0:16, p], T.dm[:], T.neye[:, p], False, True, ["dm0", "dm1"], ["x0"])
        elif what == "nt":
            ts(T.nt[0:16, :], T.x0[0:16, 0:128], T.pc[0:16, UNTIE:UNTIE + 1], None, A.add, None, ["x0", "untie"], ["nt"])
            dma("y", T.dn[r], T.nt[0:16, :], ["nt"], ["dn_own"])

    for what in ("mirror", "NW", "ahead"):
        call(0, 0, what)
    take(0, lambda: weights(0))
    weights(1)
    weights(2)
    take(1)
    for h in range(SETS):
        for what in ("places", "u0", "u1", "ahead"):
            call(h, 0, what)
    for c in range(2, len(CHUNKS)):
        take(c)
    dma("y", T.Y[:, rest + 128:], T.tl[:], ["tl", "tl_own"], ["Yrest"], 0.085 * PLAIN)
    Yk.append("Yrest")
    issue()
    turns = [(h, t) for t in range(STEPS) for h in range(SETS)]
    for n, (h, t) in enumerate(turns):
        late = tuple(x for x in TURN if x in ("*dd", "*tgt", "*dl", "*put", "*pay"))
        for x in FIRST if n == 0 else late + LAST if n == len(turns) - 1 else TURN:
            if x[0] == "sum":
                sums(h, x[1], x[2])
            elif isinstance(x, tuple):
                look(h, x[0], x[1], x[2])
            elif x[0] == "*":
                if t or x in ("*fixed", "*mirror", "*NW"):
                    call(h, max(0, t - (x != "*fixed")), x[1:])
            elif n < len(turns) - 2 or x != "ahead":
                call(turns[n - 1][0], turns[n - 1][1], x)
    for what in END:
        call(1, STEPS - 1, what)
    call(0, STEPS - 1, "store")
    to_all(T.dn[r], T.dn[r], "an", ["dn_own"], 1)
    call(1, STEPS - 1, "own")
    call(1, STEPS - 1, "store")
    dma("y", T.yi[:], T.dn[:], ["dn_own", "dn_far"], ["yi"])
    finish()
